import numpy as np
import ml_dtypes


def mxq(x, axis, fmt="e4m3"):
    dtype, down = {"e4m3": (ml_dtypes.float8_e4m3fn, 7), "e5m2": (ml_dtypes.float8_e5m2, 14)}[fmt]
    v = np.moveaxis(np.asarray(x, np.float32).astype(ml_dtypes.bfloat16).astype(np.float64), axis, -1)
    blocks = v.reshape(v.shape[:-1] + (-1, 32))
    amax = np.abs(blocks).max(-1, keepdims=True)
    byte = np.maximum(np.where(amax > 0, np.frexp(amax)[1] - 1 + 127, 0) - down, 1)
    scale = np.exp2(byte - 127.0)
    codes = (blocks / scale).astype(np.float32).astype(dtype).astype(np.float64)
    return np.moveaxis((codes * scale).reshape(v.shape), -1, axis)


WIDE = False


def mx_kscale(k):
    if not WIDE:
        return np.ones(k)
    levels = np.array([10, -10, 5, -5, 0])
    if k % 512:
        return np.exp2(np.random.permutation(np.resize(levels, k // 32))).repeat(32)
    a = np.empty((k // 512, 16))
    for p in range(k // 512):
        a[p, :8] = np.random.permutation(np.resize(levels, 8))
        for g in range(8):
            far = levels[np.abs(levels - a[p, g]) >= 10]
            a[p, g + 8] = far[np.random.randint(len(far))]
    return np.exp2(a.ravel()).repeat(32)


def f64(x):
    return np.asarray(x).astype(np.float64)


def striped(idx):
    return np.tile(idx.reshape(-1, 16).T, (8, 1)).astype(np.uint16)


def unstriped(offs):
    return offs[:16].T.reshape(-1).astype(np.int64)


E2M1 = np.array([0.0, 0.5, 1.0, 1.5, 2.0, 3.0, 4.0, 6.0, -0.0, -0.5, -1.0, -1.5, -2.0, -3.0, -4.0, -6.0])


def pack_weight(w, fmt):
    k, n = w.shape
    w = f64(np.asarray(w, np.float32).astype(ml_dtypes.bfloat16)).reshape(k // 32, 32, n)
    amax = np.abs(w).max(1)
    if fmt == "e4m3":
        byte = np.frexp(amax)[1] - 1 + 127 - 7
    else:
        mant, ex = np.frexp(amax / 6.0)
        byte = np.where(mant > 0.5, ex, ex - 1) + 127
    byte = np.clip(np.where(amax > 0, byte, 1), 1, 254)
    scaled = (w * np.exp2(127.0 - byte)[:, None, :]).reshape(k, n).astype(np.float32)
    by_word = np.ascontiguousarray(scaled.reshape(k // 512, 128, 4, n).transpose(0, 1, 3, 2))
    if fmt == "e4m3":
        words = by_word.astype(ml_dtypes.float8_e4m3fn).view(np.uint8)
    else:
        c = by_word.astype(ml_dtypes.float4_e2m1fn).view(np.uint8) & 0xF
        words = (c[..., 0::2] | (c[..., 1::2] << 4)).reshape(k // 512, 128, 2 * n)
    return np.ascontiguousarray(words), np.ascontiguousarray(byte.astype(np.uint8).reshape(k // 512, 16, n))


def unpack_weight(words, scales, fmt):
    g, _, n = scales.shape
    words = np.ascontiguousarray(words).reshape(g, 128, n, -1)
    if fmt == "e4m3":
        vals = words.view(ml_dtypes.float8_e4m3fn).astype(np.float64)
    else:
        nib = np.empty((g, 128, n, 4), np.uint8)
        nib[..., 0::2] = words & 0xF
        nib[..., 1::2] = words >> 4
        vals = E2M1[nib]
    vals = vals * np.repeat(np.exp2(scales.astype(np.float64) - 127.0), 8, axis=1)[..., None]
    return vals.transpose(0, 1, 3, 2).reshape(g * 512, n)


K, T, E, C, N = 2560, 640, 2, 256, 512
M = 384


def by_expert(wq, xq):
    return np.concatenate([wq[e].T @ xq[:, e * C:(e + 1) * C] for e in range(E)], axis=1)


def setup_inputs():
    n = np.random.standard_normal
    s = mx_kscale(K)[:, None]
    v = mx_kscale(N)
    w = [pack_weight(m, "e2m1") for m in n((E, K, N)) / np.sqrt(K) / s[None] * v[None, None, :]]
    x = pack_weight(n((K, T)) * s, "e4m3")
    return {
        "x_words": x[0],
        "x_scales": x[1],
        "w_words": np.stack([m[0] for m in w]),
        "w_scales": np.stack([m[1] for m in w]),
        "wp": (n((N, M)) / np.sqrt(N) / v[:, None]).astype(np.float32),
        "gate": np.tile(np.random.uniform(0.2, 1.0, E * C), (N, 1)).astype(np.float32),
        "offs": striped(np.random.permutation(T)[:E * C]),
    }


def reference(x_words, x_scales, w_words, w_scales, wp, gate, offs):
    idx = unstriped(offs)
    w = np.stack([unpack_weight(w_words[e], w_scales[e], "e2m1") for e in range(E)])
    xq = unpack_weight(x_words, x_scales, "e4m3")[:, idx]
    y = by_expert(w, xq)
    c = np.zeros((N, T))
    c[:, idx] = f64(gate) * y
    return mxq(f64(wp), 0, "e4m3").T @ mxq(c, 0, "e4m3")

@@ -1,0 +1,212 @@
+from contextlib import ExitStack
+
+import concourse.mybir as mybir
+from concourse.masks import make_identity
+
+K, T, E, C, N, M = 2560, 640, 2, 256, 512, 384
+FLOPS = 2 * K * N * E * C + 2 * N * M * T
+
+F32 = mybir.dt.float32
+BF16 = mybir.dt.bfloat16
+I32 = mybir.dt.int32
+U32 = mybir.dt.uint32
+U16 = mybir.dt.uint16
+U8 = mybir.dt.uint8
+FP8X4 = mybir.dt.float8_e4m3fn_x4
+FP4X4 = mybir.dt.float4_e2m1fn_x4
+COPY = mybir.ActivationFunctionType.Copy
+
+P = 128
+PASSES = K // 512
+HALVES = C // P
+FT = M // P
+OFFS_COLS = C // 16
+WP_BYTES = 4 * 4 * M
+SLOTS8 = 8
+SLOT_OF_PASS = (0, 2, 4, 6, 7)
+
+
+def tile_moe_nxt_lin_none_kernel(
+    tc, x_words, x_scales, w_words, w_scales, wp, gate, offs, out
+):
+    nc = tc.nc
+    with ExitStack() as ctx:
+        keep = ctx.enter_context(tc.tile_pool(name="keep", bufs=1))
+        late = ctx.enter_context(tc.tile_pool(name="late", bufs=1))
+        ypsum = ctx.enter_context(tc.psum_pool(name="ypsum", bufs=2))
+        tpsum = ctx.enter_context(tc.psum_pool(name="tpsum", bufs=2))
+        opsum = ctx.enter_context(tc.psum_pool(name="opsum", bufs=2))
+
+        offsets = keep.tile([P, E * OFFS_COLS], U16, name="offsets")
+        nc.sync.dma_start(offsets[:], offs)
+
+        ws = [keep.tile([P, PASSES, N], U8, name=f"ws{e}", align_bytes=64) for e in range(E)]
+        xsp = [keep.tile([P, SLOTS8, C], U8, name=f"xsp{e}", align_bytes=64) for e in range(E)]
+        windows = [keep.tile([P, T], F32, name=f"window{f}") for f in range(FT)]
+
+        def zero(t3):
+            nc.vector.memset(t3[:].rearrange("p a n -> p (a n)").bitcast(I32), 0)
+
+        zero(ws[0])
+        xs_win = keep.tile([P, T], U8, name="xs_win")
+        for b in range(2):
+            nc.scalar.dma_start(
+                xs_win[b:P:2, :].bitcast(I32),
+                x_scales[b : b + 4].rearrange("a q t -> q a t").bitcast(I32),
+            )
+
+        def load_ws(e, eng):
+            for q in range(4):
+                eng.dma_start(
+                    ws[e][32 * q : 32 * q + 4, :, :].bitcast(I32),
+                    w_scales[e, :, 4 * q : 4 * q + 4, :].rearrange("a r n -> r a n").bitcast(I32),
+                )
+
+        load_ws(0, nc.gpsimd)
+        zero(xsp[0])
+        nc.vector.memset(windows[0][:], 0.0)
+        nc.scalar.activation(windows[1][:], windows[0][:], COPY)
+        zero(ws[1])
+        zero(xsp[1])
+
+        ident = keep.tile([P, P], F32, name="ident")
+        make_identity(nc, ident[:])
+
+        x_groups = ((0, 2), (2, 4), (4, 5))
+        x_tiles = [keep.tile([P, hi - lo, T], U32, name=f"xw{lo}") for lo, hi in x_groups]
+        xw = [x_tiles[g][:, a - lo, :] for g, (lo, hi) in enumerate(x_groups) for a in range(lo, hi)]
+        ww0 = keep.tile([P, PASSES, 2 * N], U8, name="ww0", align_bytes=64)
+
+        def load_x(g):
+            lo, hi = x_groups[g]
+            nc.sync.dma_start(
+                x_tiles[g][:].bitcast(I32), x_words[lo:hi].rearrange("a p t r -> p a (t r)").bitcast(I32)
+            )
+
+        def load_w(e, tile, lo, hi):
+            nc.sync.dma_start(
+                tile[:, lo:hi, :].bitcast(I32), w_words[e, lo:hi].rearrange("a p n -> p a n").bitcast(I32)
+            )
+
+        load_x(0)
+        load_w(0, ww0, 0, 3)
+        load_x(1)
+        load_x(2)
+        load_w(0, ww0, 3, 5)
+
+        def offs_of(e):
+            return offsets[:, e * OFFS_COLS : (e + 1) * OFFS_COLS]
+
+        def gather_scales(e):
+            if e == 0:
+                xs_g = late.tile([P, C], U8, name="xs_g0", offset=WP_BYTES - 64, align_bytes=64)
+            else:
+                xs_g = keep.tile([P, C], U8, name="xs_g1")
+            nc.vector.tensor_copy(xs_g[:], xs_win[:].indirect(offs_of(e)))
+            for q in range(4):
+                nc.scalar.dma_start(
+                    xsp[e][32 * q : 32 * q + 4, :, :].bitcast(I32),
+                    xs_g[32 * q : 32 * q + 32, :].bitcast(I32),
+                )
+
+        xg = [[keep.tile([P, C], U32, name=f"xg{e}_{a}", align_bytes=64) for a in range(PASSES)] for e in range(E)]
+
+        def gather_words(e, a):
+            nc.vector.tensor_copy(xg[e][a][:], xw[a].indirect(offs_of(e)))
+
+        def expert_matmuls(e):
+            ys = [ypsum.tile([P, N], F32, name="y", tag="y") for h in range(HALVES)]
+            for a in range(PASSES):
+                for h in range(HALVES):
+                    cols = slice(h * P, (h + 1) * P)
+                    nc.tensor.matmul_mx(
+                        out=ys[h][:],
+                        lhsT=xg[e][a][:, cols].bitcast(FP8X4),
+                        lhsT_scale=xsp[e][:, SLOT_OF_PASS[a], cols],
+                        rhs=ww[e][:, a, :].bitcast(FP4X4),
+                        rhs_scale=ws[e][:, a, :],
+                        start=(a == 0),
+                        stop=(a == PASSES - 1),
+                    )
+            return ys
+
+        def quantise_c(e, ys):
+            cb = keep.tile([P, C, 4], BF16, name=f"cb{e}", align_bytes=64)
+            cb_words = cb[:].rearrange("p s t -> p (s t)").bitcast(F32)
+            for h in range(HALVES):
+                s = e * HALVES + h
+                yb = keep.tile([P, N], BF16, name=f"yb{s}")
+                nc.scalar.activation(
+                    yb[:].rearrange("s (u p d) -> s u p d", u=2, d=2),
+                    ys[h][:].rearrange("s (p u d) -> s u p d", u=2, d=2),
+                    COPY,
+                    scale=gate_col[:, s : s + 1],
+                )
+                yb_words = yb[:].bitcast(F32)
+                tp = tpsum.tile([P, 2, P], F32, name="tp", tag="tp")
+                for u in range(2):
+                    nc.tensor.transpose(tp[:, u, :], yb_words[:, u * P : (u + 1) * P], ident[:])
+                nc.scalar.copy(
+                    cb_words[:, h * 2 * P : (h + 1) * 2 * P].rearrange("p (s u) -> p s u", u=2),
+                    tp[:].rearrange("p u s -> p s u"),
+                )
+            cq = keep.tile([P, C], U32, name=f"cq{e}", align_bytes=64)
+            cs = keep.tile([P, C], U8, name=f"cs{e}", align_bytes=64)
+            nc.vector.quantize_mx(out=cq[:].bitcast(FP8X4), scales=cs[:], in_=cb[:].rearrange("p s t -> p (s t)"))
+            return cq, cs
+
+        wq = keep.tile([P, M], U32, name="wq", align_bytes=64)
+        wsc = keep.tile([P, M], U8, name="wsc", align_bytes=64)
+
+        def quantise_wp():
+            wb = keep.tile([P, M, 4], BF16, name="wb", align_bytes=64)
+            for f in range(FT):
+                cols = slice(f * P, (f + 1) * P)
+                nc.vector.tensor_copy(wb[:, cols, :], wp_raw[:, :, cols].rearrange("p j f -> p f j"))
+            for f in range(FT):
+                cols = slice(f * P, (f + 1) * P)
+                nc.vector.quantize_mx(
+                    out=wq[:, cols].bitcast(FP8X4), scales=wsc[:, cols], in_=wb[:, cols, :].rearrange("p f j -> p (f j)")
+                )
+
+        def project(e, cq, cs):
+            first = opsum.tile([P, C], F32, name="o_first", tag="o_first")
+            rest = opsum.tile([P, FT - 1, C], F32, name="o_rest", tag="o_rest")
+            dst = [first[:]] + [rest[:, f, :] for f in range(FT - 1)]
+            for f in range(FT):
+                cols = slice(f * P, (f + 1) * P)
+                nc.tensor.matmul_mx(
+                    out=dst[f], lhsT=wq[:, cols].bitcast(FP8X4), lhsT_scale=wsc[:, cols],
+                    rhs=cq[:].bitcast(FP8X4), rhs_scale=cs[:], start=True, stop=True,
+                )
+            for f in range(FT):
+                o_sb = keep.tile([P, C], F32, name=f"o_sb{e}_{f}")
+                nc.scalar.copy(o_sb[:], dst[f])
+                nc.vector.tensor_copy(windows[f][:].indirect(offs_of(e)), o_sb[:])
+                if e == E - 1:
+                    nc.sync.dma_start(out[f * P : (f + 1) * P, :], windows[f][:])
+
+        gather_scales(0)
+        gate_col = late.tile([P, E * HALVES], F32, name="gate_col", offset=WP_BYTES, align_bytes=64)
+        with nc.allow_non_contiguous_dma(reason="one gate value a slot, slots on the partitions"):
+            nc.sync.dma_start(gate_col[:], gate[0].rearrange("(s p) -> p s", p=P))
+        wp_raw = late.tile([P, 4, M], F32, name="wp_raw", offset=0, align_bytes=64)
+        nc.sync.dma_start(wp_raw[:], wp.rearrange("(p j) f -> p j f", j=4))
+        ww1 = late.tile([P, PASSES, 2 * N], U8, name="ww1", offset=WP_BYTES + 64, align_bytes=64)
+        load_w(1, ww1, 0, 3)
+        load_w(1, ww1, 3, 5)
+        ww = [ww0, ww1]
+        for a in range(PASSES):
+            gather_words(0, a)
+        ys0 = expert_matmuls(0)
+        gather_scales(1)
+        load_ws(1, nc.gpsimd)
+        nc.vector.memset(windows[2][:], 0.0)
+        quantise_wp()
+        cq0, cs0 = quantise_c(0, ys0)
+        project(0, cq0, cs0)
+        for a in range(PASSES):
+            gather_words(1, a)
+        ys1 = expert_matmuls(1)
+        cq1, cs1 = quantise_c(1, ys1)
+        project(1, cq1, cs1)

@@ -21,7 +21,10 @@ PASSES = K // 512
 HALVES = C // P
 FT = M // P
 OFFS_COLS = C // 16
-WP_BYTES = 4 * 4 * M
+WB01_AT = 0
+FIRST_COLS = 64
+Y_BANK = (0, 1, 0, 2)
+O_BANK = ((0, 2, 4), (1, 3, 1), (3, 1, 4), (3, 1, 0))
 SLOTS8 = 8
 SLOT_OF_PASS = (0, 2, 4, 6, 7)
 
@@ -33,49 +36,22 @@ def tile_moe_nxt_lin_none_kernel(
     with ExitStack() as ctx:
         keep = ctx.enter_context(tc.tile_pool(name="keep", bufs=1))
         late = ctx.enter_context(tc.tile_pool(name="late", bufs=1))
-        ypsum = ctx.enter_context(tc.psum_pool(name="ypsum", bufs=2))
-        tpsum = ctx.enter_context(tc.psum_pool(name="tpsum", bufs=2))
-        opsum = ctx.enter_context(tc.psum_pool(name="opsum", bufs=2))
-
-        offsets = keep.tile([P, E * OFFS_COLS], U16, name="offsets")
-        nc.sync.dma_start(offsets[:], offs)
-
-        ws = [keep.tile([P, PASSES, N], U8, name=f"ws{e}", align_bytes=64) for e in range(E)]
-        xsp = [keep.tile([P, SLOTS8, C], U8, name=f"xsp{e}", align_bytes=64) for e in range(E)]
-        windows = [keep.tile([P, T], F32, name=f"window{f}") for f in range(FT)]
+        banks = ctx.enter_context(tc.psum_pool(name="banks", bufs=1))
+        tpsum = ctx.enter_context(tc.psum_pool(name="tpsum", bufs=3))
 
         def zero(t3):
             nc.vector.memset(t3[:].rearrange("p a n -> p (a n)").bitcast(I32), 0)
 
-        zero(ws[0])
-        xs_win = keep.tile([P, T], U8, name="xs_win")
-        for b in range(2):
-            nc.scalar.dma_start(
-                xs_win[b:P:2, :].bitcast(I32),
-                x_scales[b : b + 4].rearrange("a q t -> q a t").bitcast(I32),
-            )
-
-        def load_ws(e, eng):
+        def load_ws(e, tile, queue):
             for q in range(4):
-                eng.dma_start(
-                    ws[e][32 * q : 32 * q + 4, :, :].bitcast(I32),
+                queue.dma_start(
+                    tile[32 * q : 32 * q + 4, :, :].bitcast(I32),
                     w_scales[e, :, 4 * q : 4 * q + 4, :].rearrange("a r n -> r a n").bitcast(I32),
                 )
-
-        load_ws(0, nc.gpsimd)
-        zero(xsp[0])
-        nc.vector.memset(windows[0][:], 0.0)
-        nc.scalar.activation(windows[1][:], windows[0][:], COPY)
-        zero(ws[1])
-        zero(xsp[1])
-
-        ident = keep.tile([P, P], F32, name="ident")
-        make_identity(nc, ident[:])
 
         x_groups = ((0, 2), (2, 4), (4, 5))
         x_tiles = [keep.tile([P, hi - lo, T], U32, name=f"xw{lo}") for lo, hi in x_groups]
         xw = [x_tiles[g][:, a - lo, :] for g, (lo, hi) in enumerate(x_groups) for a in range(lo, hi)]
-        ww0 = keep.tile([P, PASSES, 2 * N], U8, name="ww0", align_bytes=64)
 
         def load_x(g):
             lo, hi = x_groups[g]
@@ -88,125 +64,178 @@ def tile_moe_nxt_lin_none_kernel(
                 tile[:, lo:hi, :].bitcast(I32), w_words[e, lo:hi].rearrange("a p n -> p a n").bitcast(I32)
             )
 
+        ws0 = keep.tile([P, PASSES, N], U8, name="ws0", align_bytes=64)
+        ww0 = keep.tile([P, PASSES, 2 * N], U8, name="ww0", align_bytes=64)
+        xsp = [keep.tile([P, SLOTS8, C], U8, name=f"xsp{e}", align_bytes=64) for e in range(E)]
+        windows = [keep.tile([P, T], F32, name=f"window{f}") for f in range(FT)]
+        ws0_words = ws0[:].rearrange("p a n -> p (a n)").bitcast(I32)
+        nc.vector.memset(ws0_words[:, : PASSES * N // 8], 0)
+        nc.gpsimd.memset(ws0_words[:, PASSES * N // 8 :], 0)
+
+        offsets = keep.tile([P, E * OFFS_COLS], U16, name="offsets")
+        nc.sync.dma_start(offsets[:], offs)
+        xs_win = keep.tile([P, T], U8, name="xs_win")
+        for b in range(2):
+            nc.sync.dma_start(
+                xs_win[b:P:2, :].bitcast(I32),
+                x_scales[b : b + 4].rearrange("a q t -> q a t").bitcast(I32),
+            )
         load_x(0)
-        load_w(0, ww0, 0, 3)
+        load_ws(0, ws0, nc.scalar)
+        load_w(0, ww0, 0, 5)
         load_x(1)
         load_x(2)
-        load_w(0, ww0, 3, 5)
 
-        def offs_of(e):
-            return offsets[:, e * OFFS_COLS : (e + 1) * OFFS_COLS]
+        zero(xsp[0])
+        nc.vector.memset(windows[0][:], 0.0)
+        nc.scalar.activation(windows[1][:, :FIRST_COLS], windows[0][:, :FIRST_COLS], COPY)
+        zero(xsp[1])
+        ws1 = keep.tile([P, PASSES, N], U8, name="ws1", align_bytes=64)
+        zero(ws1)
+        gate_col = keep.tile([P, E * HALVES], F32, name="gate_col")
+        with nc.allow_non_contiguous_dma(reason="one gate value a slot, slots on the partitions"):
+            nc.gpsimd.dma_start(gate_col[:], gate[0].rearrange("(s p) -> p s", p=P))
+        ident = keep.tile([P, P], F32, name="ident")
+        make_identity(nc, ident[:])
 
-        def gather_scales(e):
-            if e == 0:
-                xs_g = late.tile([P, C], U8, name="xs_g0", offset=WP_BYTES - 64, align_bytes=64)
-            else:
-                xs_g = keep.tile([P, C], U8, name="xs_g1")
-            nc.vector.tensor_copy(xs_g[:], xs_win[:].indirect(offs_of(e)))
+        def offs_of(lo, hi):
+            return offsets[:, lo * P // 16 : hi * P // 16]
+
+        def gather_scales(e, xs_g):
+            nc.vector.tensor_copy(xs_g[:], xs_win[:].indirect(offs_of(HALVES * e, HALVES * (e + 1))))
             for q in range(4):
                 nc.scalar.dma_start(
                     xsp[e][32 * q : 32 * q + 4, :, :].bitcast(I32),
                     xs_g[32 * q : 32 * q + 32, :].bitcast(I32),
                 )
 
+        xs_g0 = keep.tile([P, C], U8, name="xs_g0")
+        xs_g1 = keep.tile([P, C], U8, name="xs_g1")
+        gather_scales(0, xs_g0)
+        nc.scalar.activation(windows[1][:, FIRST_COLS:], windows[0][:, FIRST_COLS:], COPY)
+        nc.scalar.activation(windows[2][:], windows[0][:], COPY)
+        gather_scales(1, xs_g1)
+
+        wp_raw = keep.tile([P, 4, M], F32, name="wp_raw")
+        wp_rows_hbm = wp.rearrange("(p j) f -> p j f", j=4)
+        nc.sync.dma_start(wp_raw[:, :, : 2 * P], wp_rows_hbm[:, :, : 2 * P])
+        ww1 = keep.tile([P, PASSES, 2 * N], U8, name="ww1", align_bytes=64)
+        load_w(1, ww1, 0, 3)
+        load_w(1, ww1, 3, 5)
+        load_ws(1, ws1, nc.sync)
+        nc.sync.dma_start(wp_raw[:, :, 2 * P :], wp_rows_hbm[:, :, 2 * P :])
+        ww = [ww0, ww1]
+
         xg = [[keep.tile([P, C], U32, name=f"xg{e}_{a}", align_bytes=64) for a in range(PASSES)] for e in range(E)]
+        xg_first = late.tile([P, P], U32, name="xg_first", offset=WB01_AT, align_bytes=64)
+
+        def gathered(s, a):
+            e, h = divmod(s, HALVES)
+            if (s, a) == (0, PASSES - 1):
+                return xg_first[:]
+            return xg[e][a][:, h * P : (h + 1) * P]
 
         def gather_words(e, a):
-            nc.vector.tensor_copy(xg[e][a][:], xw[a].indirect(offs_of(e)))
+            nc.vector.tensor_copy(xg[e][a][:], xw[a].indirect(offs_of(HALVES * e, HALVES * (e + 1))))
 
-        def expert_matmuls(e):
-            ys = [ypsum.tile([P, N], F32, name="y", tag="y") for h in range(HALVES)]
+        def expert_matmuls(s, ws):
+            e, h = divmod(s, HALVES)
+            cols = slice(h * P, (h + 1) * P)
+            y = banks.tile([P, N], F32, name="y", tag=f"bank{Y_BANK[s]}")
             for a in range(PASSES):
-                for h in range(HALVES):
-                    cols = slice(h * P, (h + 1) * P)
-                    nc.tensor.matmul_mx(
-                        out=ys[h][:],
-                        lhsT=xg[e][a][:, cols].bitcast(FP8X4),
-                        lhsT_scale=xsp[e][:, SLOT_OF_PASS[a], cols],
-                        rhs=ww[e][:, a, :].bitcast(FP4X4),
-                        rhs_scale=ws[e][:, a, :],
-                        start=(a == 0),
-                        stop=(a == PASSES - 1),
-                    )
-            return ys
+                nc.tensor.matmul_mx(
+                    out=y[:],
+                    lhsT=gathered(s, a).bitcast(FP8X4),
+                    lhsT_scale=xsp[e][:, SLOT_OF_PASS[a], cols],
+                    rhs=ww[e][:, a, :].bitcast(FP4X4),
+                    rhs_scale=ws[:, a, :],
+                    start=(a == 0),
+                    stop=(a == PASSES - 1),
+                )
+            return y
 
-        def quantise_c(e, ys):
-            cb = keep.tile([P, C, 4], BF16, name=f"cb{e}", align_bytes=64)
-            cb_words = cb[:].rearrange("p s t -> p (s t)").bitcast(F32)
-            for h in range(HALVES):
-                s = e * HALVES + h
-                yb = keep.tile([P, N], BF16, name=f"yb{s}")
-                nc.scalar.activation(
-                    yb[:].rearrange("s (u p d) -> s u p d", u=2, d=2),
-                    ys[h][:].rearrange("s (p u d) -> s u p d", u=2, d=2),
-                    COPY,
-                    scale=gate_col[:, s : s + 1],
-                )
-                yb_words = yb[:].bitcast(F32)
-                tp = tpsum.tile([P, 2, P], F32, name="tp", tag="tp")
-                for u in range(2):
-                    nc.tensor.transpose(tp[:, u, :], yb_words[:, u * P : (u + 1) * P], ident[:])
-                nc.scalar.copy(
-                    cb_words[:, h * 2 * P : (h + 1) * 2 * P].rearrange("p (s u) -> p s u", u=2),
-                    tp[:].rearrange("p u s -> p s u"),
-                )
-            cq = keep.tile([P, C], U32, name=f"cq{e}", align_bytes=64)
-            cs = keep.tile([P, C], U8, name=f"cs{e}", align_bytes=64)
-            nc.vector.quantize_mx(out=cq[:].bitcast(FP8X4), scales=cs[:], in_=cb[:].rearrange("p s t -> p (s t)"))
-            return cq, cs
+        def gate_and_round(s, y):
+            yb = keep.tile([P, N], BF16, name=f"yb{s}")
+            nc.scalar.activation(
+                yb[:].rearrange("s (u p d) -> s u p d", u=2, d=2),
+                y[:].rearrange("s (p u d) -> s u p d", u=2, d=2),
+                COPY,
+                scale=gate_col[:, s : s + 1],
+            )
+            return yb
+
+        def turn(yb, cb_words):
+            yb_words = yb[:].bitcast(F32)
+            tp = tpsum.tile([P, 2, P], F32, name="tp", tag="tp")
+            for u in range(2):
+                nc.tensor.transpose(tp[:, u, :], yb_words[:, u * P : (u + 1) * P], ident[:])
+            nc.scalar.copy(cb_words.rearrange("p (s u) -> p s u", u=2), tp[:].rearrange("p u s -> p s u"))
+
+        cq = keep.tile([P, E * C], U32, name="cq", align_bytes=64)
+        cs = keep.tile([P, E * C], U8, name="cs", align_bytes=64)
+
+        def quantise_c(s, yb):
+            cols = slice(s * P, (s + 1) * P)
+            cb = keep.tile([P, 4 * P], BF16, name=f"cb{s}", align_bytes=64)
+            turn(yb, cb[:].bitcast(F32))
+            nc.vector.quantize_mx(out=cq[:, cols].bitcast(FP8X4), scales=cs[:, cols], in_=cb[:])
 
         wq = keep.tile([P, M], U32, name="wq", align_bytes=64)
         wsc = keep.tile([P, M], U8, name="wsc", align_bytes=64)
 
-        def quantise_wp():
-            wb = keep.tile([P, M, 4], BF16, name="wb", align_bytes=64)
-            for f in range(FT):
-                cols = slice(f * P, (f + 1) * P)
-                nc.vector.tensor_copy(wb[:, cols, :], wp_raw[:, :, cols].rearrange("p j f -> p f j"))
-            for f in range(FT):
-                cols = slice(f * P, (f + 1) * P)
-                nc.vector.quantize_mx(
-                    out=wq[:, cols].bitcast(FP8X4), scales=wsc[:, cols], in_=wb[:, cols, :].rearrange("p f j -> p (f j)")
-                )
+        def wp_rows(f):
+            return wp_raw[:, :, f * P : (f + 1) * P].rearrange("p j f -> p f j")
 
-        def project(e, cq, cs):
-            first = opsum.tile([P, C], F32, name="o_first", tag="o_first")
-            rest = opsum.tile([P, FT - 1, C], F32, name="o_rest", tag="o_rest")
-            dst = [first[:]] + [rest[:, f, :] for f in range(FT - 1)]
-            for f in range(FT):
-                cols = slice(f * P, (f + 1) * P)
-                nc.tensor.matmul_mx(
-                    out=dst[f], lhsT=wq[:, cols].bitcast(FP8X4), lhsT_scale=wsc[:, cols],
-                    rhs=cq[:].bitcast(FP8X4), rhs_scale=cs[:], start=True, stop=True,
-                )
-            for f in range(FT):
-                o_sb = keep.tile([P, C], F32, name=f"o_sb{e}_{f}")
-                nc.scalar.copy(o_sb[:], dst[f])
-                nc.vector.tensor_copy(windows[f][:].indirect(offs_of(e)), o_sb[:])
-                if e == E - 1:
-                    nc.sync.dma_start(out[f * P : (f + 1) * P, :], windows[f][:])
+        def quantise_wp(lo, hi, wb):
+            cols = slice(lo * P, hi * P)
+            nc.vector.quantize_mx(
+                out=wq[:, cols].bitcast(FP8X4), scales=wsc[:, cols], in_=wb[:].rearrange("p f j -> p (f j)")
+            )
 
-        gather_scales(0)
-        gate_col = late.tile([P, E * HALVES], F32, name="gate_col", offset=WP_BYTES, align_bytes=64)
-        with nc.allow_non_contiguous_dma(reason="one gate value a slot, slots on the partitions"):
-            nc.sync.dma_start(gate_col[:], gate[0].rearrange("(s p) -> p s", p=P))
-        wp_raw = late.tile([P, 4, M], F32, name="wp_raw", offset=0, align_bytes=64)
-        nc.sync.dma_start(wp_raw[:], wp.rearrange("(p j) f -> p j f", j=4))
-        ww1 = late.tile([P, PASSES, 2 * N], U8, name="ww1", offset=WP_BYTES + 64, align_bytes=64)
-        load_w(1, ww1, 0, 3)
-        load_w(1, ww1, 3, 5)
-        ww = [ww0, ww1]
-        for a in range(PASSES):
-            gather_words(0, a)
-        ys0 = expert_matmuls(0)
-        gather_scales(1)
-        load_ws(1, nc.gpsimd)
-        nc.vector.memset(windows[2][:], 0.0)
-        quantise_wp()
-        cq0, cs0 = quantise_c(0, ys0)
-        project(0, cq0, cs0)
-        for a in range(PASSES):
+        def project(s, f):
+            slots = slice(s * P, (s + 1) * P)
+            cols = slice(f * P, (f + 1) * P)
+            o = banks.tile([P, P], F32, name="o", tag=f"bank{O_BANK[s][f]}")
+            nc.tensor.matmul_mx(
+                out=o[:], lhsT=wq[:, cols].bitcast(FP8X4), lhsT_scale=wsc[:, cols],
+                rhs=cq[:, slots].bitcast(FP8X4), rhs_scale=cs[:, slots], start=True, stop=True,
+            )
+            o_sb = keep.tile([P, P], F32, name=f"o_sb{s}_{f}")
+            nc.scalar.copy(o_sb[:], o[:])
+            nc.vector.tensor_copy(windows[f][:].indirect(offs_of(s, s + 1)), o_sb[:])
+            if s == E * HALVES - 1:
+                nc.sync.dma_start(out[f * P : (f + 1) * P, :], windows[f][:])
+
+        for e, a in ((0, 0), (0, 1), (1, 0), (1, 1), (0, 2), (0, 3)):
+            gather_words(e, a)
+        for s in range(HALVES):
+            nc.vector.tensor_copy(gathered(s, PASSES - 1), xw[PASSES - 1].indirect(offs_of(s, s + 1)))
+        for a in range(2, PASSES):
             gather_words(1, a)
-        ys1 = expert_matmuls(1)
-        cq1, cs1 = quantise_c(1, ys1)
-        project(1, cq1, cs1)
+
+        yb0 = gate_and_round(0, expert_matmuls(0, ws0))
+        wb01 = late.tile([P, 2 * P, 4], BF16, name="wb01", offset=WB01_AT, align_bytes=64)
+        nc.vector.tensor_copy(wb01[:, :P, :], wp_rows(0))
+        nc.scalar.copy(wb01[:, P:, :], wp_rows(1))
+        quantise_wp(0, 2, wb01)
+        quantise_c(0, yb0)
+        yb1 = gate_and_round(1, expert_matmuls(1, ws0))
+        project(0, 0)
+        project(0, 1)
+        quantise_c(1, yb1)
+        project(1, 0)
+        project(1, 1)
+        wb2 = keep.tile([P, P, 4], BF16, name="wb2", align_bytes=64)
+        nc.scalar.copy(wb2[:], wp_rows(2))
+        quantise_wp(2, 3, wb2)
+        yb2 = gate_and_round(2, expert_matmuls(2, ws1))
+        project(0, 2)
+        quantise_c(2, yb2)
+        yb3 = gate_and_round(3, expert_matmuls(3, ws1))
+        project(1, 2)
+        project(2, 0)
+        quantise_c(3, yb3)
+        project(2, 1)
+        project(2, 2)
+        for f in range(FT):
+            project(3, f)

@@ -17,16 +17,20 @@ FP4X4 = mybir.dt.float4_e2m1fn_x4
 COPY = mybir.ActivationFunctionType.Copy
 
 P = 128
-PASSES = K // 512
-HALVES = C // P
-FT = M // P
-OFFS_COLS = C // 16
-WB01_AT = 0
-FIRST_COLS = 64
-Y_BANK = (0, 1, 0, 2)
-O_BANK = ((0, 2, 4), (1, 3, 1), (3, 1, 4), (3, 1, 0))
-SLOTS8 = 8
-SLOT_OF_PASS = (0, 2, 4, 6, 7)
+PACK = 4
+PASSES = K // (P * PACK)
+TILES_PER_EXPERT = C // P
+SLOT_TILES = E * TILES_PER_EXPERT
+FEATURE_TILES = M // P
+LIST_COLS = P // 16
+
+X_FIRST = 2
+W_FIRST = 3
+WARM_PASSES = 2
+QUADRANTS = (0, 2, 1, 3)
+PLANES = 8
+PLANE_OF_PASS = (0, 2, 4, 6, 7)
+SCALE_PAD = 64
 
 
 def tile_moe_nxt_lin_none_kernel(
@@ -35,207 +39,178 @@ def tile_moe_nxt_lin_none_kernel(
     nc = tc.nc
     with ExitStack() as ctx:
         keep = ctx.enter_context(tc.tile_pool(name="keep", bufs=1))
-        late = ctx.enter_context(tc.tile_pool(name="late", bufs=1))
         banks = ctx.enter_context(tc.psum_pool(name="banks", bufs=1))
-        tpsum = ctx.enter_context(tc.psum_pool(name="tpsum", bufs=3))
+        turned = ctx.enter_context(tc.psum_pool(name="turned", bufs=3))
 
-        def zero(t3):
-            nc.vector.memset(t3[:].rearrange("p a n -> p (a n)").bitcast(I32), 0)
+        def zero(planes, engine):
+            engine.memset(planes.rearrange("p a n -> p (a n)").bitcast(I32), 0)
 
-        def load_ws(e, tile, queue):
-            for q in range(4):
-                queue.dma_start(
-                    tile[32 * q : 32 * q + 4, :, :].bitcast(I32),
-                    w_scales[e, :, 4 * q : 4 * q + 4, :].rearrange("a r n -> r a n").bitcast(I32),
-                )
+        def slot_offsets(lo, hi):
+            return offsets[:, lo * LIST_COLS : hi * LIST_COLS]
 
-        x_groups = ((0, 2), (2, 4), (4, 5))
-        x_tiles = [keep.tile([P, hi - lo, T], U32, name=f"xw{lo}") for lo, hi in x_groups]
-        xw = [x_tiles[g][:, a - lo, :] for g, (lo, hi) in enumerate(x_groups) for a in range(lo, hi)]
-
-        def load_x(g):
-            lo, hi = x_groups[g]
+        def load_weights(e, lo, hi):
             nc.sync.dma_start(
-                x_tiles[g][:].bitcast(I32), x_words[lo:hi].rearrange("a p t r -> p a (t r)").bitcast(I32)
+                w_sb[e][:, lo:hi, :].bitcast(I32), w_words[e, lo:hi].rearrange("a p n -> p a n").bitcast(I32)
             )
 
-        def load_w(e, tile, lo, hi):
-            nc.sync.dma_start(
-                tile[:, lo:hi, :].bitcast(I32), w_words[e, lo:hi].rearrange("a p n -> p a n").bitcast(I32)
-            )
+        w_planes = keep.tile([P, E * PASSES, N], U8, name="w_planes", align_bytes=64)
+        x_planes = keep.tile([P, PLANES, E * C], U8, name="x_planes", align_bytes=64)
+        w_sb = [keep.tile([P, PASSES, 2 * N], U8, name=f"w_sb{e}", align_bytes=64) for e in range(E)]
+        windows = [keep.tile([P, T], F32, name=f"window{f}") for f in range(FEATURE_TILES)]
+        zero(w_planes[:, :PASSES, :], nc.vector)
+        zero(w_planes[:, PASSES:, :], nc.gpsimd)
 
-        ws0 = keep.tile([P, PASSES, N], U8, name="ws0", align_bytes=64)
-        ww0 = keep.tile([P, PASSES, 2 * N], U8, name="ww0", align_bytes=64)
-        xsp = [keep.tile([P, SLOTS8, C], U8, name=f"xsp{e}", align_bytes=64) for e in range(E)]
-        windows = [keep.tile([P, T], F32, name=f"window{f}") for f in range(FT)]
-        ws0_words = ws0[:].rearrange("p a n -> p (a n)").bitcast(I32)
-        nc.vector.memset(ws0_words[:, : PASSES * N // 8], 0)
-        nc.gpsimd.memset(ws0_words[:, PASSES * N // 8 :], 0)
-
-        offsets = keep.tile([P, E * OFFS_COLS], U16, name="offsets")
+        offsets = keep.tile([P, SLOT_TILES * LIST_COLS], U16, name="offsets")
         nc.sync.dma_start(offsets[:], offs)
-        xs_win = keep.tile([P, T], U8, name="xs_win")
+        xs_window = keep.tile([P, T + SCALE_PAD], U8, name="xs_window")
+        nc.gpsimd.memset(xs_window[:, T:], 0)
         for b in range(2):
             nc.sync.dma_start(
-                xs_win[b:P:2, :].bitcast(I32),
-                x_scales[b : b + 4].rearrange("a q t -> q a t").bitcast(I32),
+                xs_window[b:P:2, :T].bitcast(I32),
+                x_scales[b : b + PASSES - 1].rearrange("a q t -> q a t").bitcast(I32),
             )
-        load_x(0)
-        load_ws(0, ws0, nc.scalar)
-        load_w(0, ww0, 0, 5)
-        load_x(1)
-        load_x(2)
+        x_pass = []
+        for lo, hi in ((0, X_FIRST), (X_FIRST, PASSES)):
+            x_sb = keep.tile([P, hi - lo, T], U32, name=f"x_sb{lo}")
+            nc.sync.dma_start(x_sb[:].bitcast(I32), x_words[lo:hi].rearrange("a p t r -> p a (t r)").bitcast(I32))
+            x_pass.extend(x_sb[:, a, :] for a in range(hi - lo))
+        for q in QUADRANTS:
+            nc.sync.dma_start(
+                w_planes[32 * q : 32 * q + 4, :, :].bitcast(I32),
+                w_scales[:, :, 4 * q : 4 * q + 4, :].rearrange("e a r n -> r (e a) n").bitcast(I32),
+            )
+        load_weights(0, 0, W_FIRST)
 
-        zero(xsp[0])
+        zero(x_planes[:, : PLANES // 2, :], nc.vector)
+        zero(x_planes[:, PLANES // 2 :, :], nc.gpsimd)
         nc.vector.memset(windows[0][:], 0.0)
-        nc.scalar.activation(windows[1][:, :FIRST_COLS], windows[0][:, :FIRST_COLS], COPY)
-        zero(xsp[1])
-        ws1 = keep.tile([P, PASSES, N], U8, name="ws1", align_bytes=64)
-        zero(ws1)
-        gate_col = keep.tile([P, E * HALVES], F32, name="gate_col")
-        with nc.allow_non_contiguous_dma(reason="one gate value a slot, slots on the partitions"):
-            nc.gpsimd.dma_start(gate_col[:], gate[0].rearrange("(s p) -> p s", p=P))
+        for f in range(1, FEATURE_TILES):
+            nc.scalar.activation(windows[f][:], windows[0][:], COPY)
         ident = keep.tile([P, P], F32, name="ident")
         make_identity(nc, ident[:])
 
-        def offs_of(lo, hi):
-            return offsets[:, lo * P // 16 : hi * P // 16]
+        xs_gathered = keep.tile([P, E * C], U8, name="xs_gathered", align_bytes=64)
+        nc.vector.tensor_copy(xs_gathered[:], xs_window[:].indirect(offsets[:]))
+        for q in QUADRANTS:
+            nc.sync.dma_start(
+                x_planes[32 * q : 32 * q + 4, :, :].bitcast(I32), xs_gathered[32 * q : 32 * q + 32, :].bitcast(I32)
+            )
+        load_weights(0, W_FIRST, PASSES)
+        gate_col = keep.tile([P, SLOT_TILES], F32, name="gate_col")
+        with nc.allow_non_contiguous_dma(reason="one gate value a slot, slots on the partitions"):
+            nc.sync.dma_start(gate_col[:], gate[0].rearrange("(s p) -> p s", p=P))
+        wp_by_row = wp.rearrange("(p j) f -> p j f", j=PACK)
+        wp_raw = keep.tile([P, PACK, M], F32, name="wp_raw")
+        nc.sync.dma_start(wp_raw[:, :, :P], wp_by_row[:, :, :P])
+        load_weights(1, 0, PASSES)
+        nc.sync.dma_start(wp_raw[:, :, P:], wp_by_row[:, :, P:])
 
-        def gather_scales(e, xs_g):
-            nc.vector.tensor_copy(xs_g[:], xs_win[:].indirect(offs_of(HALVES * e, HALVES * (e + 1))))
-            for q in range(4):
-                nc.scalar.dma_start(
-                    xsp[e][32 * q : 32 * q + 4, :, :].bitcast(I32),
-                    xs_g[32 * q : 32 * q + 32, :].bitcast(I32),
-                )
+        x_gathered = {}
+        for lo, hi in ((0, X_FIRST), (X_FIRST, PASSES)):
+            for e in range(E):
+                for a in range(lo, hi):
+                    words = keep.tile([P, C], U32, name=f"x_gathered{e}_{a}", align_bytes=64)
+                    slots = slot_offsets(e * TILES_PER_EXPERT, (e + 1) * TILES_PER_EXPERT)
+                    nc.vector.tensor_copy(words[:], x_pass[a].indirect(slots))
+                    x_gathered[e, a] = words
 
-        xs_g0 = keep.tile([P, C], U8, name="xs_g0")
-        xs_g1 = keep.tile([P, C], U8, name="xs_g1")
-        gather_scales(0, xs_g0)
-        nc.scalar.activation(windows[1][:, FIRST_COLS:], windows[0][:, FIRST_COLS:], COPY)
-        nc.scalar.activation(windows[2][:], windows[0][:], COPY)
-        gather_scales(1, xs_g1)
+        warm = banks.tile([P, N], F32, name="warm", tag="bank4")
+        for a in range(WARM_PASSES):
+            nc.tensor.matmul_mx(
+                out=warm[:],
+                lhsT=x_gathered[0, a][:, :P].bitcast(FP8X4),
+                lhsT_scale=xs_gathered[:, :P],
+                rhs=w_sb[0][:, a, :].bitcast(FP4X4),
+                rhs_scale=w_planes[:, a, :],
+                start=True,
+                stop=True,
+            )
 
-        wp_raw = keep.tile([P, 4, M], F32, name="wp_raw")
-        wp_rows_hbm = wp.rearrange("(p j) f -> p j f", j=4)
-        nc.sync.dma_start(wp_raw[:, :, : 2 * P], wp_rows_hbm[:, :, : 2 * P])
-        ww1 = keep.tile([P, PASSES, 2 * N], U8, name="ww1", align_bytes=64)
-        load_w(1, ww1, 0, 3)
-        load_w(1, ww1, 3, 5)
-        load_ws(1, ws1, nc.sync)
-        nc.sync.dma_start(wp_raw[:, :, 2 * P :], wp_rows_hbm[:, :, 2 * P :])
-        ww = [ww0, ww1]
-
-        xg = [[keep.tile([P, C], U32, name=f"xg{e}_{a}", align_bytes=64) for a in range(PASSES)] for e in range(E)]
-        xg_first = late.tile([P, P], U32, name="xg_first", offset=WB01_AT, align_bytes=64)
-
-        def gathered(s, a):
-            e, h = divmod(s, HALVES)
-            if (s, a) == (0, PASSES - 1):
-                return xg_first[:]
-            return xg[e][a][:, h * P : (h + 1) * P]
-
-        def gather_words(e, a):
-            nc.vector.tensor_copy(xg[e][a][:], xw[a].indirect(offs_of(HALVES * e, HALVES * (e + 1))))
-
-        def expert_matmuls(s, ws):
-            e, h = divmod(s, HALVES)
-            cols = slice(h * P, (h + 1) * P)
-            y = banks.tile([P, N], F32, name="y", tag=f"bank{Y_BANK[s]}")
+        def gated_expert(s):
+            e, h = divmod(s, TILES_PER_EXPERT)
+            y = banks.tile([P, N], F32, name="y", tag=f"bank{h}")
             for a in range(PASSES):
                 nc.tensor.matmul_mx(
                     out=y[:],
-                    lhsT=gathered(s, a).bitcast(FP8X4),
-                    lhsT_scale=xsp[e][:, SLOT_OF_PASS[a], cols],
-                    rhs=ww[e][:, a, :].bitcast(FP4X4),
-                    rhs_scale=ws[:, a, :],
+                    lhsT=x_gathered[e, a][:, h * P : (h + 1) * P].bitcast(FP8X4),
+                    lhsT_scale=x_planes[:, PLANE_OF_PASS[a], s * P : (s + 1) * P],
+                    rhs=w_sb[e][:, a, :].bitcast(FP4X4),
+                    rhs_scale=w_planes[:, e * PASSES + a, :],
                     start=(a == 0),
                     stop=(a == PASSES - 1),
                 )
-            return y
-
-        def gate_and_round(s, y):
-            yb = keep.tile([P, N], BF16, name=f"yb{s}")
+            c_by_slot = keep.tile([P, N], BF16, name=f"c_by_slot{s}")
             nc.scalar.activation(
-                yb[:].rearrange("s (u p d) -> s u p d", u=2, d=2),
+                c_by_slot[:].rearrange("s (u p d) -> s u p d", u=2, d=2),
                 y[:].rearrange("s (p u d) -> s u p d", u=2, d=2),
                 COPY,
                 scale=gate_col[:, s : s + 1],
             )
-            return yb
+            return c_by_slot
 
-        def turn(yb, cb_words):
-            yb_words = yb[:].bitcast(F32)
-            tp = tpsum.tile([P, 2, P], F32, name="tp", tag="tp")
-            for u in range(2):
-                nc.tensor.transpose(tp[:, u, :], yb_words[:, u * P : (u + 1) * P], ident[:])
-            nc.scalar.copy(cb_words.rearrange("p (s u) -> p s u", u=2), tp[:].rearrange("p u s -> p s u"))
+        c_codes = keep.tile([P, E * C], U32, name="c_codes", align_bytes=64)
+        c_scales = keep.tile([P, E * C], U8, name="c_scales", align_bytes=64)
 
-        cq = keep.tile([P, E * C], U32, name="cq", align_bytes=64)
-        cs = keep.tile([P, E * C], U8, name="cs", align_bytes=64)
+        def quantise_c(lo, tiles, tag):
+            c_by_n = keep.tile([P, len(tiles) * P * PACK], BF16, name=f"c_by_n{lo}", tag=tag, align_bytes=64)
+            for i, c_by_slot in enumerate(tiles):
+                pairs = turned.tile([P, 2, P], F32, name="pairs", tag="pairs")
+                for u in range(2):
+                    nc.tensor.transpose(pairs[:, u, :], c_by_slot[:].bitcast(F32)[:, u * P : (u + 1) * P], ident[:])
+                nc.scalar.copy(
+                    c_by_n[:].bitcast(F32)[:, i * 2 * P : (i + 1) * 2 * P].rearrange("p (s u) -> p s u", u=2),
+                    pairs[:].rearrange("p u s -> p s u"),
+                )
+            slots = slice(lo * P, (lo + len(tiles)) * P)
+            nc.vector.quantize_mx(out=c_codes[:, slots].bitcast(FP8X4), scales=c_scales[:, slots], in_=c_by_n[:])
 
-        def quantise_c(s, yb):
-            cols = slice(s * P, (s + 1) * P)
-            cb = keep.tile([P, 4 * P], BF16, name=f"cb{s}", align_bytes=64)
-            turn(yb, cb[:].bitcast(F32))
-            nc.vector.quantize_mx(out=cq[:, cols].bitcast(FP8X4), scales=cs[:, cols], in_=cb[:])
+        wp_codes = keep.tile([P, M], U32, name="wp_codes", align_bytes=64)
+        wp_scales = keep.tile([P, M], U8, name="wp_scales", align_bytes=64)
 
-        wq = keep.tile([P, M], U32, name="wq", align_bytes=64)
-        wsc = keep.tile([P, M], U8, name="wsc", align_bytes=64)
-
-        def wp_rows(f):
-            return wp_raw[:, :, f * P : (f + 1) * P].rearrange("p j f -> p f j")
-
-        def quantise_wp(lo, hi, wb):
-            cols = slice(lo * P, hi * P)
-            nc.vector.quantize_mx(
-                out=wq[:, cols].bitcast(FP8X4), scales=wsc[:, cols], in_=wb[:].rearrange("p f j -> p (f j)")
-            )
-
-        def project(s, f):
-            slots = slice(s * P, (s + 1) * P)
+        def quantise_wp(f, copy):
             cols = slice(f * P, (f + 1) * P)
-            o = banks.tile([P, P], F32, name="o", tag=f"bank{O_BANK[s][f]}")
-            nc.tensor.matmul_mx(
-                out=o[:], lhsT=wq[:, cols].bitcast(FP8X4), lhsT_scale=wsc[:, cols],
-                rhs=cq[:, slots].bitcast(FP8X4), rhs_scale=cs[:, slots], start=True, stop=True,
+            wp_bf = keep.tile([P, P, PACK], BF16, name=f"wp_bf{f}", align_bytes=64)
+            copy(wp_bf[:], wp_raw[:, :, cols].rearrange("p j f -> p f j"))
+            nc.vector.quantize_mx(
+                out=wp_codes[:, cols].bitcast(FP8X4),
+                scales=wp_scales[:, cols],
+                in_=wp_bf[:].rearrange("p f j -> p (f j)"),
             )
-            o_sb = keep.tile([P, P], F32, name=f"o_sb{s}_{f}")
+
+        def project(lo, hi, f, bank, tag):
+            slots = slice(lo * P, hi * P)
+            cols = slice(f * P, (f + 1) * P)
+            o = banks.tile([P, (hi - lo) * P], F32, name="o", tag=f"bank{bank}")
+            nc.tensor.matmul_mx(
+                out=o[:],
+                lhsT=wp_codes[:, cols].bitcast(FP8X4),
+                lhsT_scale=wp_scales[:, cols],
+                rhs=c_codes[:, slots].bitcast(FP8X4),
+                rhs_scale=c_scales[:, slots],
+                start=True,
+                stop=True,
+            )
+            o_sb = keep.tile([P, (hi - lo) * P], F32, name=f"o_sb{lo}_{f}", tag=tag, align_bytes=64)
             nc.scalar.copy(o_sb[:], o[:])
-            nc.vector.tensor_copy(windows[f][:].indirect(offs_of(s, s + 1)), o_sb[:])
-            if s == E * HALVES - 1:
-                nc.sync.dma_start(out[f * P : (f + 1) * P, :], windows[f][:])
+            nc.vector.tensor_copy(windows[f][:].indirect(slot_offsets(lo, hi)), o_sb[:])
+            if hi == SLOT_TILES:
+                nc.sync.dma_start(out[cols, :], windows[f][:])
 
-        for e, a in ((0, 0), (0, 1), (1, 0), (1, 1), (0, 2), (0, 3)):
-            gather_words(e, a)
-        for s in range(HALVES):
-            nc.vector.tensor_copy(gathered(s, PASSES - 1), xw[PASSES - 1].indirect(offs_of(s, s + 1)))
-        for a in range(2, PASSES):
-            gather_words(1, a)
+        c0 = gated_expert(0)
+        c1 = gated_expert(1)
+        quantise_wp(0, nc.vector.tensor_copy)
+        quantise_c(0, [c0], "c_by_n0")
+        quantise_c(1, [c1], "c_by_n1")
+        project(0, 1, 0, bank=2, tag="o_0_0")
+        quantise_wp(1, nc.scalar.copy)
+        project(1, 2, 0, bank=3, tag="o_1_0")
+        project(0, 2, 1, bank=4, tag="o_0_1")
 
-        yb0 = gate_and_round(0, expert_matmuls(0, ws0))
-        wb01 = late.tile([P, 2 * P, 4], BF16, name="wb01", offset=WB01_AT, align_bytes=64)
-        nc.vector.tensor_copy(wb01[:, :P, :], wp_rows(0))
-        nc.scalar.copy(wb01[:, P:, :], wp_rows(1))
-        quantise_wp(0, 2, wb01)
-        quantise_c(0, yb0)
-        yb1 = gate_and_round(1, expert_matmuls(1, ws0))
-        project(0, 0)
-        project(0, 1)
-        quantise_c(1, yb1)
-        project(1, 0)
-        project(1, 1)
-        wb2 = keep.tile([P, P, 4], BF16, name="wb2", align_bytes=64)
-        nc.scalar.copy(wb2[:], wp_rows(2))
-        quantise_wp(2, 3, wb2)
-        yb2 = gate_and_round(2, expert_matmuls(2, ws1))
-        project(0, 2)
-        quantise_c(2, yb2)
-        yb3 = gate_and_round(3, expert_matmuls(3, ws1))
-        project(1, 2)
-        project(2, 0)
-        quantise_c(3, yb3)
-        project(2, 1)
-        project(2, 2)
-        for f in range(FT):
-            project(3, f)
+        c2 = gated_expert(2)
+        quantise_wp(2, nc.scalar.copy)
+        c3 = gated_expert(3)
+        quantise_c(2, [c2, c3], "shared")
+        project(0, 2, 2, bank=2, tag="shared")
+        project(2, 4, 0, bank=0, tag="o_2_0")
+        project(2, 4, 1, bank=1, tag="o_2_1")
+        project(2, 4, 2, bank=3, tag="o_2_2")

@@ -22,11 +22,13 @@ PASSES = K // (P * PACK)
 TILES_PER_EXPERT = C // P
 SLOT_TILES = E * TILES_PER_EXPERT
 FEATURE_TILES = M // P
+TOKEN_TILES = T // P
+BANKS = 6
 LIST_COLS = P // 16
 
 X_FIRST = 2
 W_FIRST = 3
-WARM_PASSES = 2
+WARM_PASSES = 8
 QUADRANTS = (0, 2, 1, 3)
 PLANES = 8
 PLANE_OF_PASS = (0, 2, 4, 6, 7)
@@ -40,7 +42,7 @@ def tile_moe_nxt_lin_none_kernel(
     with ExitStack() as ctx:
         keep = ctx.enter_context(tc.tile_pool(name="keep", bufs=1))
         banks = ctx.enter_context(tc.psum_pool(name="banks", bufs=1))
-        turned = ctx.enter_context(tc.psum_pool(name="turned", bufs=3))
+        turned = ctx.enter_context(tc.psum_pool(name="turned", bufs=2))
 
         def zero(planes, engine):
             engine.memset(planes.rearrange("p a n -> p (a n)").bitcast(I32), 0)
@@ -48,15 +50,33 @@ def tile_moe_nxt_lin_none_kernel(
         def slot_offsets(lo, hi):
             return offsets[:, lo * LIST_COLS : hi * LIST_COLS]
 
+        def load_weight_scales(e):
+            for q in QUADRANTS:
+                nc.sync.dma_start(
+                    w_planes[32 * q : 32 * q + 4, e * PASSES : (e + 1) * PASSES, :].bitcast(I32),
+                    w_scales[e, :, 4 * q : 4 * q + 4, :].rearrange("a r n -> r a n").bitcast(I32),
+                )
+
+        def move_token_scales(e):
+            for q in QUADRANTS:
+                nc.sync.dma_start(
+                    x_planes[e][32 * q : 32 * q + 4, :, :].bitcast(I32),
+                    xs_gathered[32 * q : 32 * q + 32, e * C : (e + 1) * C].bitcast(I32),
+                )
+
         def load_weights(e, lo, hi):
             nc.sync.dma_start(
                 w_sb[e][:, lo:hi, :].bitcast(I32), w_words[e, lo:hi].rearrange("a p n -> p a n").bitcast(I32)
             )
 
         w_planes = keep.tile([P, E * PASSES, N], U8, name="w_planes", align_bytes=64)
-        x_planes = keep.tile([P, PLANES, E * C], U8, name="x_planes", align_bytes=64)
+        x_planes = [keep.tile([P, PLANES, C], U8, name=f"x_planes{e}", align_bytes=64) for e in range(E)]
         w_sb = [keep.tile([P, PASSES, 2 * N], U8, name=f"w_sb{e}", align_bytes=64) for e in range(E)]
-        windows = [keep.tile([P, T], F32, name=f"window{f}") for f in range(FEATURE_TILES)]
+        windows = [keep.tile([P, T], F32, name=f"window{u}") for u in range(2)]
+        gate_rows = keep.tile([P, P], F32, name="gate_rows")
+        zero_col = keep.tile([P, 1], F32, name="zero_col")
+        nc.vector.memset(zero_col[:], 0.0)
+        nc.vector.memset(gate_rows[:], 0.0)
         zero(w_planes[:, :PASSES, :], nc.vector)
         zero(w_planes[:, PASSES:, :], nc.gpsimd)
 
@@ -74,36 +94,31 @@ def tile_moe_nxt_lin_none_kernel(
             x_sb = keep.tile([P, hi - lo, T], U32, name=f"x_sb{lo}")
             nc.sync.dma_start(x_sb[:].bitcast(I32), x_words[lo:hi].rearrange("a p t r -> p a (t r)").bitcast(I32))
             x_pass.extend(x_sb[:, a, :] for a in range(hi - lo))
-        for q in QUADRANTS:
-            nc.sync.dma_start(
-                w_planes[32 * q : 32 * q + 4, :, :].bitcast(I32),
-                w_scales[:, :, 4 * q : 4 * q + 4, :].rearrange("e a r n -> r (e a) n").bitcast(I32),
-            )
-        load_weights(0, 0, W_FIRST)
-
-        zero(x_planes[:, : PLANES // 2, :], nc.vector)
-        zero(x_planes[:, PLANES // 2 :, :], nc.gpsimd)
-        nc.vector.memset(windows[0][:], 0.0)
-        for f in range(1, FEATURE_TILES):
-            nc.scalar.activation(windows[f][:], windows[0][:], COPY)
+            if lo == 0:
+                load_weight_scales(0)
         ident = keep.tile([P, P], F32, name="ident")
         make_identity(nc, ident[:])
+        nc.sync.dma_start(gate_rows[:SLOT_TILES, :], gate[0].rearrange("(s p) -> s p", p=P))
+        zero(x_planes[0][:], nc.vector)
+        zero(x_planes[1][:], nc.gpsimd)
+        for u in range(2):
+            nc.scalar.copy(windows[u][:], zero_col[:].to_broadcast([P, T]))
+        gate_turned = banks.tile([P, P], F32, name="gate_turned", tag="bank5")
+        nc.tensor.transpose(gate_turned[:], gate_rows[:], ident[:])
+        gate_col = keep.tile([P, SLOT_TILES], F32, name="gate_col")
+        nc.scalar.copy(gate_col[:], gate_turned[:, :SLOT_TILES])
 
         xs_gathered = keep.tile([P, E * C], U8, name="xs_gathered", align_bytes=64)
         nc.vector.tensor_copy(xs_gathered[:], xs_window[:].indirect(offsets[:]))
-        for q in QUADRANTS:
-            nc.sync.dma_start(
-                x_planes[32 * q : 32 * q + 4, :, :].bitcast(I32), xs_gathered[32 * q : 32 * q + 32, :].bitcast(I32)
-            )
+        load_weights(0, 0, W_FIRST)
+        move_token_scales(0)
         load_weights(0, W_FIRST, PASSES)
-        gate_col = keep.tile([P, SLOT_TILES], F32, name="gate_col")
-        with nc.allow_non_contiguous_dma(reason="one gate value a slot, slots on the partitions"):
-            nc.sync.dma_start(gate_col[:], gate[0].rearrange("(s p) -> p s", p=P))
-        wp_by_row = wp.rearrange("(p j) f -> p j f", j=PACK)
+        load_weight_scales(1)
+        move_token_scales(1)
+        load_weights(1, 0, W_FIRST)
+        load_weights(1, W_FIRST, PASSES)
         wp_raw = keep.tile([P, PACK, M], F32, name="wp_raw")
-        nc.sync.dma_start(wp_raw[:, :, :P], wp_by_row[:, :, :P])
-        load_weights(1, 0, PASSES)
-        nc.sync.dma_start(wp_raw[:, :, P:], wp_by_row[:, :, P:])
+        nc.sync.dma_start(wp_raw[:], wp.rearrange("(p j) f -> p j f", j=PACK))
 
         x_gathered = {}
         for lo, hi in ((0, X_FIRST), (X_FIRST, PASSES)):
@@ -114,103 +129,101 @@ def tile_moe_nxt_lin_none_kernel(
                     nc.vector.tensor_copy(words[:], x_pass[a].indirect(slots))
                     x_gathered[e, a] = words
 
-        warm = banks.tile([P, N], F32, name="warm", tag="bank4")
+        warm = banks.tile([P, C], F32, name="warm", tag="bank4")
+        warm_words = x_gathered[1, X_FIRST - 1]
         for a in range(WARM_PASSES):
             nc.tensor.matmul_mx(
                 out=warm[:],
-                lhsT=x_gathered[0, a][:, :P].bitcast(FP8X4),
+                lhsT=warm_words[:, :P].bitcast(FP8X4),
                 lhsT_scale=xs_gathered[:, :P],
-                rhs=w_sb[0][:, a, :].bitcast(FP4X4),
-                rhs_scale=w_planes[:, a, :],
+                rhs=warm_words[:].bitcast(FP8X4),
+                rhs_scale=xs_gathered[:, :C],
                 start=True,
                 stop=True,
             )
 
-        def gated_expert(s):
+        c_pairs = [keep.tile([P, 2, C], F32, name=f"c_pairs{e}") for e in range(E)]
+
+        def gated_expert(s, parts):
             e, h = divmod(s, TILES_PER_EXPERT)
-            y = banks.tile([P, N], F32, name="y", tag=f"bank{h}")
+            y = banks.tile([P, N], F32, name="y", tag=f"bank{s}")
             for a in range(PASSES):
                 nc.tensor.matmul_mx(
                     out=y[:],
                     lhsT=x_gathered[e, a][:, h * P : (h + 1) * P].bitcast(FP8X4),
-                    lhsT_scale=x_planes[:, PLANE_OF_PASS[a], s * P : (s + 1) * P],
+                    lhsT_scale=x_planes[e][:, PLANE_OF_PASS[a], h * P : (h + 1) * P],
                     rhs=w_sb[e][:, a, :].bitcast(FP4X4),
                     rhs_scale=w_planes[:, e * PASSES + a, :],
                     start=(a == 0),
                     stop=(a == PASSES - 1),
                 )
-            c_by_slot = keep.tile([P, N], BF16, name=f"c_by_slot{s}")
-            nc.scalar.activation(
-                c_by_slot[:].rearrange("s (u p d) -> s u p d", u=2, d=2),
-                y[:].rearrange("s (p u d) -> s u p d", u=2, d=2),
-                COPY,
-                scale=gate_col[:, s : s + 1],
+            c_by_slot = keep.tile([P, 2, P, 2], BF16, name=f"c_by_slot{s}", tag=f"stage{s}", align_bytes=64)
+            y_by_u = y[:].rearrange("s (p u d) -> s u p d", u=2, d=2)
+            for us in parts:
+                nc.scalar.activation(c_by_slot[:, us], y_by_u[:, us], COPY, scale=gate_col[:, s : s + 1])
+            for us in parts:
+                pairs = turned.tile([P, us.stop - us.start, P], F32, name="pairs", tag="pairs")
+                for u in range(us.start, us.stop):
+                    words = c_by_slot[:, u].rearrange("s p d -> s (p d)").bitcast(F32)
+                    nc.tensor.transpose(pairs[:, u - us.start, :], words, ident[:])
+                nc.scalar.copy(c_pairs[e][:, us, h * P : (h + 1) * P], pairs[:])
+
+        def scatter(u, lo, hi):
+            e, h = divmod(lo, TILES_PER_EXPERT)
+            nc.vector.tensor_copy(
+                windows[u][:].indirect(slot_offsets(lo, hi)), c_pairs[e][:, u, h * P : (h + hi - lo) * P]
             )
-            return c_by_slot
-
-        c_codes = keep.tile([P, E * C], U32, name="c_codes", align_bytes=64)
-        c_scales = keep.tile([P, E * C], U8, name="c_scales", align_bytes=64)
-
-        def quantise_c(lo, tiles, tag):
-            c_by_n = keep.tile([P, len(tiles) * P * PACK], BF16, name=f"c_by_n{lo}", tag=tag, align_bytes=64)
-            for i, c_by_slot in enumerate(tiles):
-                pairs = turned.tile([P, 2, P], F32, name="pairs", tag="pairs")
-                for u in range(2):
-                    nc.tensor.transpose(pairs[:, u, :], c_by_slot[:].bitcast(F32)[:, u * P : (u + 1) * P], ident[:])
-                nc.scalar.copy(
-                    c_by_n[:].bitcast(F32)[:, i * 2 * P : (i + 1) * 2 * P].rearrange("p (s u) -> p s u", u=2),
-                    pairs[:].rearrange("p u s -> p s u"),
-                )
-            slots = slice(lo * P, (lo + len(tiles)) * P)
-            nc.vector.quantize_mx(out=c_codes[:, slots].bitcast(FP8X4), scales=c_scales[:, slots], in_=c_by_n[:])
 
         wp_codes = keep.tile([P, M], U32, name="wp_codes", align_bytes=64)
         wp_scales = keep.tile([P, M], U8, name="wp_scales", align_bytes=64)
 
-        def quantise_wp(f, copy):
-            cols = slice(f * P, (f + 1) * P)
-            wp_bf = keep.tile([P, P, PACK], BF16, name=f"wp_bf{f}", align_bytes=64)
-            copy(wp_bf[:], wp_raw[:, :, cols].rearrange("p j f -> p f j"))
+        def quantise_wp(lo, hi):
+            cols = slice(lo * P, hi * P)
+            wp_bf = keep.tile([P, (hi - lo) * P, PACK], BF16, name=f"wp_bf{lo}", tag=f"stage{lo + 1}", align_bytes=64)
+            nc.scalar.copy(wp_bf[:], wp_raw[:, :, cols].rearrange("p j f -> p f j"))
             nc.vector.quantize_mx(
                 out=wp_codes[:, cols].bitcast(FP8X4),
                 scales=wp_scales[:, cols],
                 in_=wp_bf[:].rearrange("p f j -> p (f j)"),
             )
 
-        def project(lo, hi, f, bank, tag):
-            slots = slice(lo * P, hi * P)
-            cols = slice(f * P, (f + 1) * P)
-            o = banks.tile([P, (hi - lo) * P], F32, name="o", tag=f"bank{bank}")
-            nc.tensor.matmul_mx(
-                out=o[:],
-                lhsT=wp_codes[:, cols].bitcast(FP8X4),
-                lhsT_scale=wp_scales[:, cols],
-                rhs=c_codes[:, slots].bitcast(FP8X4),
-                rhs_scale=c_scales[:, slots],
-                start=True,
-                stop=True,
-            )
-            o_sb = keep.tile([P, (hi - lo) * P], F32, name=f"o_sb{lo}_{f}", tag=tag, align_bytes=64)
-            nc.scalar.copy(o_sb[:], o[:])
-            nc.vector.tensor_copy(windows[f][:].indirect(slot_offsets(lo, hi)), o_sb[:])
-            if hi == SLOT_TILES:
-                nc.sync.dma_start(out[cols, :], windows[f][:])
+        for s in range(SLOT_TILES):
+            gated_expert(s, (slice(0, 1), slice(1, 2)) if s in (0, SLOT_TILES - 1) else (slice(0, 2),))
+            scatter(0, s, s + 1)
+            scatter(1, s, s + 1)
+        for f in range(FEATURE_TILES):
+            quantise_wp(f, f + 1)
 
-        c0 = gated_expert(0)
-        c1 = gated_expert(1)
-        quantise_wp(0, nc.vector.tensor_copy)
-        quantise_c(0, [c0], "c_by_n0")
-        quantise_c(1, [c1], "c_by_n1")
-        project(0, 1, 0, bank=2, tag="o_0_0")
-        quantise_wp(1, nc.scalar.copy)
-        project(1, 2, 0, bank=3, tag="o_1_0")
-        project(0, 2, 1, bank=4, tag="o_0_1")
+        c_by_token = [keep.tile([P, P * PACK], BF16, name=f"c_by_token{i}", align_bytes=64) for i in range(TOKEN_TILES)]
+        c_words = [c[:].bitcast(F32).rearrange("p (t u) -> p t u", u=2) for c in c_by_token]
+        for i in range(TOKEN_TILES):
+            nc.scalar.copy(c_words[i], windows[0][:, i * P : (i + 1) * P].unsqueeze(2).to_broadcast([P, P, 2]))
 
-        c2 = gated_expert(2)
-        quantise_wp(2, nc.scalar.copy)
-        c3 = gated_expert(3)
-        quantise_c(2, [c2, c3], "shared")
-        project(0, 2, 2, bank=2, tag="shared")
-        project(2, 4, 0, bank=0, tag="o_2_0")
-        project(2, 4, 1, bank=1, tag="o_2_1")
-        project(2, 4, 2, bank=3, tag="o_2_2")
+        def weave(i):
+            nc.vector.tensor_copy(c_words[i][:, :, 1], windows[1][:, i * P : (i + 1) * P])
+
+        def project(i):
+            codes = keep.tile([P, P], U32, name=f"c_codes{i}", align_bytes=64)
+            scales = keep.tile([P, P], U8, name=f"c_scales{i}", align_bytes=64)
+            nc.vector.quantize_mx(out=codes[:].bitcast(FP8X4), scales=scales[:], in_=c_by_token[i][:])
+            o = banks.tile([P, FEATURE_TILES, P], F32, name="o", tag=f"bank{(i + SLOT_TILES) % BANKS}")
+            for f in range(FEATURE_TILES):
+                cols = slice(f * P, (f + 1) * P)
+                nc.tensor.matmul_mx(
+                    out=o[:, f, :],
+                    lhsT=wp_codes[:, cols].bitcast(FP8X4),
+                    lhsT_scale=wp_scales[:, cols],
+                    rhs=codes[:].bitcast(FP8X4),
+                    rhs_scale=scales[:],
+                    start=True,
+                    stop=True,
+                )
+            o_sb = keep.tile([P, FEATURE_TILES, P], F32, name=f"o_sb{i}")
+            (nc.vector.tensor_copy if i == TOKEN_TILES - 2 else nc.scalar.copy)(o_sb[:], o[:])
+            nc.sync.dma_start(out.rearrange("(f p) t -> p f t", p=P)[:, :, i * P : (i + 1) * P], o_sb[:])
+
+        weave(0)
+        for i in range(TOKEN_TILES):
+            if i + 1 < TOKEN_TILES:
+                weave(i + 1)
+            project(i)

@@ -28,6 +28,11 @@ LIST_COLS = P // 16
 
 X_FIRST = 2
 W_FIRST = 3
+SPLIT = (0, 1, 2, 3)
+WARM_ON = (1, 0)
+VCOPY = (3,)
+VPAIR = ((0, 0), (0, 1))
+FIRST = ((0, 1), (1, 3))
 WARM_PASSES = 8
 QUADRANTS = (0, 2, 1, 3)
 PLANES = 8
@@ -130,7 +135,7 @@ def tile_moe_nxt_lin_none_kernel(
                     x_gathered[e, a] = words
 
         warm = banks.tile([P, C], F32, name="warm", tag="bank4")
-        warm_words = x_gathered[1, X_FIRST - 1]
+        warm_words = x_gathered[WARM_ON]
         for a in range(WARM_PASSES):
             nc.tensor.matmul_mx(
                 out=warm[:],
@@ -166,7 +171,7 @@ def tile_moe_nxt_lin_none_kernel(
                 for u in range(us.start, us.stop):
                     words = c_by_slot[:, u].rearrange("s p d -> s (p d)").bitcast(F32)
                     nc.tensor.transpose(pairs[:, u - us.start, :], words, ident[:])
-                nc.scalar.copy(c_pairs[e][:, us, h * P : (h + 1) * P], pairs[:])
+                (nc.vector.tensor_copy if (s, us.start) in VPAIR else nc.scalar.copy)(c_pairs[e][:, us, h * P : (h + 1) * P], pairs[:])
 
         def scatter(u, lo, hi):
             e, h = divmod(lo, TILES_PER_EXPERT)
@@ -188,7 +193,7 @@ def tile_moe_nxt_lin_none_kernel(
             )
 
         for s in range(SLOT_TILES):
-            gated_expert(s, (slice(0, 1), slice(1, 2)) if s in (0, SLOT_TILES - 1) else (slice(0, 2),))
+            gated_expert(s, (slice(0, 1), slice(1, 2)) if s in SPLIT else (slice(0, 2),))
             scatter(0, s, s + 1)
             scatter(1, s, s + 1)
         for f in range(FEATURE_TILES):
@@ -206,22 +211,24 @@ def tile_moe_nxt_lin_none_kernel(
             codes = keep.tile([P, P], U32, name=f"c_codes{i}", align_bytes=64)
             scales = keep.tile([P, P], U8, name=f"c_scales{i}", align_bytes=64)
             nc.vector.quantize_mx(out=codes[:].bitcast(FP8X4), scales=scales[:], in_=c_by_token[i][:])
-            o = banks.tile([P, FEATURE_TILES, P], F32, name="o", tag=f"bank{(i + SLOT_TILES) % BANKS}")
-            for f in range(FEATURE_TILES):
-                cols = slice(f * P, (f + 1) * P)
-                nc.tensor.matmul_mx(
-                    out=o[:, f, :],
-                    lhsT=wp_codes[:, cols].bitcast(FP8X4),
-                    lhsT_scale=wp_scales[:, cols],
-                    rhs=codes[:].bitcast(FP8X4),
-                    rhs_scale=scales[:],
-                    start=True,
-                    stop=True,
-                )
-            o_sb = keep.tile([P, FEATURE_TILES, P], F32, name=f"o_sb{i}")
-            (nc.vector.tensor_copy if i == TOKEN_TILES - 2 else nc.scalar.copy)(o_sb[:], o[:])
-            nc.sync.dma_start(out.rearrange("(f p) t -> p f t", p=P)[:, :, i * P : (i + 1) * P], o_sb[:])
+            for lo, hi in FIRST if i == 0 else ((0, FEATURE_TILES),):
+                o = banks.tile([P, hi - lo, P], F32, name="o", tag=f"bank{bank_order.pop(0)}")
+                for f in range(lo, hi):
+                    cols = slice(f * P, (f + 1) * P)
+                    nc.tensor.matmul_mx(
+                        out=o[:, f - lo, :],
+                        lhsT=wp_codes[:, cols].bitcast(FP8X4),
+                        lhsT_scale=wp_scales[:, cols],
+                        rhs=codes[:].bitcast(FP8X4),
+                        rhs_scale=scales[:],
+                        start=True,
+                        stop=True,
+                    )
+                o_sb = keep.tile([P, hi - lo, P], F32, name=f"o_sb{i}_{lo}")
+                (nc.vector.tensor_copy if i in VCOPY else nc.scalar.copy)(o_sb[:], o[:])
+                nc.sync.dma_start(out.rearrange("(f p) t -> p f t", p=P)[:, lo:hi, i * P : (i + 1) * P], o_sb[:])
 
+        bank_order = [4, 5, 0, 1, 2, 3]
         weave(0)
         for i in range(TOKEN_TILES):
             if i + 1 < TOKEN_TILES:

@@ -28,12 +28,10 @@ LIST_COLS = P // 16
 
 X_FIRST = 2
 W_FIRST = 3
-SPLIT = (0, 1, 2, 3)
-WARM_ON = (1, 0)
+WARM = ((1, 1, 8),)
+MID = 3
 VCOPY = (3,)
-VPAIR = ((0, 0), (0, 1))
 FIRST = ((0, 1), (1, 3))
-WARM_PASSES = 8
 QUADRANTS = (0, 2, 1, 3)
 PLANES = 8
 PLANE_OF_PASS = (0, 2, 4, 6, 7)
@@ -47,7 +45,7 @@ def tile_moe_nxt_lin_none_kernel(
     with ExitStack() as ctx:
         keep = ctx.enter_context(tc.tile_pool(name="keep", bufs=1))
         banks = ctx.enter_context(tc.psum_pool(name="banks", bufs=1))
-        turned = ctx.enter_context(tc.psum_pool(name="turned", bufs=2))
+        turned = ctx.enter_context(tc.psum_pool(name="turned", bufs=4))
 
         def zero(planes, engine):
             engine.memset(planes.rearrange("p a n -> p (a n)").bitcast(I32), 0)
@@ -108,7 +106,7 @@ def tile_moe_nxt_lin_none_kernel(
         zero(x_planes[1][:], nc.gpsimd)
         for u in range(2):
             nc.scalar.copy(windows[u][:], zero_col[:].to_broadcast([P, T]))
-        gate_turned = banks.tile([P, P], F32, name="gate_turned", tag="bank5")
+        gate_turned = banks.tile([P, P], F32, name="gate_turned", tag="bank3")
         nc.tensor.transpose(gate_turned[:], gate_rows[:], ident[:])
         gate_col = keep.tile([P, SLOT_TILES], F32, name="gate_col")
         nc.scalar.copy(gate_col[:], gate_turned[:, :SLOT_TILES])
@@ -134,24 +132,27 @@ def tile_moe_nxt_lin_none_kernel(
                     nc.vector.tensor_copy(words[:], x_pass[a].indirect(slots))
                     x_gathered[e, a] = words
 
-        warm = banks.tile([P, C], F32, name="warm", tag="bank4")
-        warm_words = x_gathered[WARM_ON]
-        for a in range(WARM_PASSES):
-            nc.tensor.matmul_mx(
-                out=warm[:],
-                lhsT=warm_words[:, :P].bitcast(FP8X4),
-                lhsT_scale=xs_gathered[:, :P],
-                rhs=warm_words[:].bitcast(FP8X4),
-                rhs_scale=xs_gathered[:, :C],
-                start=True,
-                stop=True,
-            )
+        def warm_up(words, passes, bank):
+            warm = banks.tile([P, C], F32, name="warm", tag=bank)
+            for i in range(passes):
+                nc.tensor.matmul_mx(
+                    out=warm[:],
+                    lhsT=words[:, :P].bitcast(FP8X4),
+                    lhsT_scale=xs_gathered[:, :P],
+                    rhs=words[:].bitcast(FP8X4),
+                    rhs_scale=xs_gathered[:, :C],
+                    start=True,
+                    stop=True,
+                )
 
-        c_pairs = [keep.tile([P, 2, C], F32, name=f"c_pairs{e}") for e in range(E)]
+        for e, a, passes in WARM:
+            warm_up(x_gathered[e, a], passes, "bank2")
 
-        def gated_expert(s, parts):
+        c_pairs = {(s, u): keep.tile([P, P], F32, name=f"c_pairs{s}_{u}") for s in range(SLOT_TILES) for u in range(2)}
+
+        def gated_expert(s):
             e, h = divmod(s, TILES_PER_EXPERT)
-            y = banks.tile([P, N], F32, name="y", tag=f"bank{s}")
+            y = banks.tile([P, N], F32, name="y", tag=f"bank{h}")
             for a in range(PASSES):
                 nc.tensor.matmul_mx(
                     out=y[:],
@@ -162,21 +163,23 @@ def tile_moe_nxt_lin_none_kernel(
                     start=(a == 0),
                     stop=(a == PASSES - 1),
                 )
-            c_by_slot = keep.tile([P, 2, P, 2], BF16, name=f"c_by_slot{s}", tag=f"stage{s}", align_bytes=64)
             y_by_u = y[:].rearrange("s (p u d) -> s u p d", u=2, d=2)
-            for us in parts:
-                nc.scalar.activation(c_by_slot[:, us], y_by_u[:, us], COPY, scale=gate_col[:, s : s + 1])
-            for us in parts:
-                pairs = turned.tile([P, us.stop - us.start, P], F32, name="pairs", tag="pairs")
-                for u in range(us.start, us.stop):
-                    words = c_by_slot[:, u].rearrange("s p d -> s (p d)").bitcast(F32)
-                    nc.tensor.transpose(pairs[:, u - us.start, :], words, ident[:])
-                (nc.vector.tensor_copy if (s, us.start) in VPAIR else nc.scalar.copy)(c_pairs[e][:, us, h * P : (h + 1) * P], pairs[:])
+            halves = []
+            for u in range(2):
+                half = keep.tile([P, 2 * P], BF16, name=f"c_by_slot{s}_{u}", tag=f"stage{s}_{u}", align_bytes=64)
+                nc.scalar.activation(
+                    half[:].rearrange("s (p d) -> s p d", d=2), y_by_u[:, u], COPY, scale=gate_col[:, s : s + 1]
+                )
+                halves.append(half)
+            for u in range(2):
+                pairs = turned.tile([P, P], F32, name="pairs", tag="pairs")
+                nc.tensor.transpose(pairs[:], halves[u][:].bitcast(F32), ident[:])
+                nc.scalar.copy(c_pairs[s, u][:], pairs[:])
 
         def scatter(u, lo, hi):
             e, h = divmod(lo, TILES_PER_EXPERT)
             nc.vector.tensor_copy(
-                windows[u][:].indirect(slot_offsets(lo, hi)), c_pairs[e][:, u, h * P : (h + hi - lo) * P]
+                windows[u][:].indirect(slot_offsets(lo, hi)), c_pairs[lo, u][:]
             )
 
         wp_codes = keep.tile([P, M], U32, name="wp_codes", align_bytes=64)
@@ -184,7 +187,7 @@ def tile_moe_nxt_lin_none_kernel(
 
         def quantise_wp(lo, hi):
             cols = slice(lo * P, hi * P)
-            wp_bf = keep.tile([P, (hi - lo) * P, PACK], BF16, name=f"wp_bf{lo}", tag=f"stage{lo + 1}", align_bytes=64)
+            wp_bf = keep.tile([P, (hi - lo) * P, PACK], BF16, name=f"wp_bf{lo}", tag=f"stage{lo + 1}_1", align_bytes=64)
             nc.scalar.copy(wp_bf[:], wp_raw[:, :, cols].rearrange("p j f -> p f j"))
             nc.vector.quantize_mx(
                 out=wp_codes[:, cols].bitcast(FP8X4),
@@ -193,9 +196,11 @@ def tile_moe_nxt_lin_none_kernel(
             )
 
         for s in range(SLOT_TILES):
-            gated_expert(s, (slice(0, 1), slice(1, 2)) if s in SPLIT else (slice(0, 2),))
+            gated_expert(s)
             scatter(0, s, s + 1)
             scatter(1, s, s + 1)
+            if s == 1 and MID:
+                warm_up(x_gathered[0, 0], MID, "bank0")
         for f in range(FEATURE_TILES):
             quantise_wp(f, f + 1)
 
@@ -228,7 +233,7 @@ def tile_moe_nxt_lin_none_kernel(
                 (nc.vector.tensor_copy if i in VCOPY else nc.scalar.copy)(o_sb[:], o[:])
                 nc.sync.dma_start(out.rearrange("(f p) t -> p f t", p=P)[:, lo:hi, i * P : (i + 1) * P], o_sb[:])
 
-        bank_order = [4, 5, 0, 1, 2, 3]
+        bank_order = [2, 3, 0, 1, 2, 3]
         weave(0)
         for i in range(TOKEN_TILES):
             if i + 1 < TOKEN_TILES:

@@ -27,9 +27,10 @@ BANKS = 6
 LIST_COLS = P // 16
 
 X_FIRST = 2
-W_FIRST = 3
+W_FIRST = 2
+W1_FIRST = 3
 WARM = ((1, 1, 8),)
-MID = 3
+MID = 2
 VCOPY = (3,)
 FIRST = ((0, 1), (1, 3))
 QUADRANTS = (0, 2, 1, 3)
@@ -97,8 +98,7 @@ def tile_moe_nxt_lin_none_kernel(
             x_sb = keep.tile([P, hi - lo, T], U32, name=f"x_sb{lo}")
             nc.sync.dma_start(x_sb[:].bitcast(I32), x_words[lo:hi].rearrange("a p t r -> p a (t r)").bitcast(I32))
             x_pass.extend(x_sb[:, a, :] for a in range(hi - lo))
-            if lo == 0:
-                load_weight_scales(0)
+        load_weight_scales(0)
         ident = keep.tile([P, P], F32, name="ident")
         make_identity(nc, ident[:])
         nc.sync.dma_start(gate_rows[:SLOT_TILES, :], gate[0].rearrange("(s p) -> s p", p=P))
@@ -118,8 +118,8 @@ def tile_moe_nxt_lin_none_kernel(
         load_weights(0, W_FIRST, PASSES)
         load_weight_scales(1)
         move_token_scales(1)
-        load_weights(1, 0, W_FIRST)
-        load_weights(1, W_FIRST, PASSES)
+        load_weights(1, 0, W1_FIRST)
+        load_weights(1, W1_FIRST, PASSES)
         wp_raw = keep.tile([P, PACK, M], F32, name="wp_raw")
         nc.sync.dma_start(wp_raw[:], wp.rearrange("(p j) f -> p j f", j=PACK))
 

@@ -31,8 +31,8 @@ W_FIRST = 2
 W1_FIRST = 3
 WARM = ((1, 1, 8),)
 MID = 2
-VCOPY = (3,)
-FIRST = ((0, 1), (1, 3))
+VCOPY = ((2, 0), (2, 2))
+TOKEN_RUNS = ((0, 128), (128, 384), (384, 640))
 QUADRANTS = (0, 2, 1, 3)
 PLANES = 8
 PLANE_OF_PASS = (0, 2, 4, 6, 7)
@@ -204,38 +204,40 @@ def tile_moe_nxt_lin_none_kernel(
         for f in range(FEATURE_TILES):
             quantise_wp(f, f + 1)
 
-        c_by_token = [keep.tile([P, P * PACK], BF16, name=f"c_by_token{i}", align_bytes=64) for i in range(TOKEN_TILES)]
+        c_by_token = [
+            keep.tile([P, (hi - lo) * PACK], BF16, name=f"c_by_token{lo}", align_bytes=64) for lo, hi in TOKEN_RUNS
+        ]
         c_words = [c[:].bitcast(F32).rearrange("p (t u) -> p t u", u=2) for c in c_by_token]
-        for i in range(TOKEN_TILES):
-            nc.scalar.copy(c_words[i], windows[0][:, i * P : (i + 1) * P].unsqueeze(2).to_broadcast([P, P, 2]))
+        for words, (lo, hi) in zip(c_words, TOKEN_RUNS):
+            nc.scalar.copy(words, windows[0][:, lo:hi].unsqueeze(2).to_broadcast([P, hi - lo, 2]))
 
         def weave(i):
-            nc.vector.tensor_copy(c_words[i][:, :, 1], windows[1][:, i * P : (i + 1) * P])
+            lo, hi = TOKEN_RUNS[i]
+            nc.vector.tensor_copy(c_words[i][:, :, 1], windows[1][:, lo:hi])
 
         def project(i):
-            codes = keep.tile([P, P], U32, name=f"c_codes{i}", align_bytes=64)
-            scales = keep.tile([P, P], U8, name=f"c_scales{i}", align_bytes=64)
+            lo, hi = TOKEN_RUNS[i]
+            codes = keep.tile([P, hi - lo], U32, name=f"c_codes{i}", align_bytes=64)
+            scales = keep.tile([P, hi - lo], U8, name=f"c_scales{i}", align_bytes=64)
             nc.vector.quantize_mx(out=codes[:].bitcast(FP8X4), scales=scales[:], in_=c_by_token[i][:])
-            for lo, hi in FIRST if i == 0 else ((0, FEATURE_TILES),):
-                o = banks.tile([P, hi - lo, P], F32, name="o", tag=f"bank{bank_order.pop(0)}")
-                for f in range(lo, hi):
-                    cols = slice(f * P, (f + 1) * P)
-                    nc.tensor.matmul_mx(
-                        out=o[:, f - lo, :],
-                        lhsT=wp_codes[:, cols].bitcast(FP8X4),
-                        lhsT_scale=wp_scales[:, cols],
-                        rhs=codes[:].bitcast(FP8X4),
-                        rhs_scale=scales[:],
-                        start=True,
-                        stop=True,
-                    )
-                o_sb = keep.tile([P, hi - lo, P], F32, name=f"o_sb{i}_{lo}")
-                (nc.vector.tensor_copy if i in VCOPY else nc.scalar.copy)(o_sb[:], o[:])
-                nc.sync.dma_start(out.rearrange("(f p) t -> p f t", p=P)[:, lo:hi, i * P : (i + 1) * P], o_sb[:])
+            for f in range(FEATURE_TILES):
+                cols = slice(f * P, (f + 1) * P)
+                o = turned.tile([P, hi - lo], F32, name="o", tag="pairs")
+                nc.tensor.matmul_mx(
+                    out=o[:],
+                    lhsT=wp_codes[:, cols].bitcast(FP8X4),
+                    lhsT_scale=wp_scales[:, cols],
+                    rhs=codes[:].bitcast(FP8X4),
+                    rhs_scale=scales[:],
+                    start=True,
+                    stop=True,
+                )
+                o_sb = keep.tile([P, hi - lo], F32, name=f"o_sb{i}_{f}")
+                (nc.vector.tensor_copy if (i, f) in VCOPY else nc.scalar.copy)(o_sb[:], o[:])
+                nc.sync.dma_start(out[cols, lo:hi], o_sb[:])
 
-        bank_order = [2, 3, 0, 1, 2, 3]
         weave(0)
-        for i in range(TOKEN_TILES):
-            if i + 1 < TOKEN_TILES:
+        for i in range(len(TOKEN_RUNS)):
+            if i + 1 < len(TOKEN_RUNS):
                 weave(i + 1)
             project(i)

@@ -34,8 +34,6 @@ MID = 2
 VCOPY = ((2, 0), (2, 2))
 TOKEN_RUNS = ((0, 128), (128, 384), (384, 640))
 QUADRANTS = (0, 2, 1, 3)
-PLANES = 8
-PLANE_OF_PASS = (0, 2, 4, 6, 7)
 SCALE_PAD = 64
 
 
@@ -61,11 +59,18 @@ def tile_moe_nxt_lin_none_kernel(
                     w_scales[e, :, 4 * q : 4 * q + 4, :].rearrange("a r n -> r a n").bitcast(I32),
                 )
 
-        def move_token_scales(e):
+        def move_token_scales():
             for q in QUADRANTS:
                 nc.sync.dma_start(
-                    x_planes[e][32 * q : 32 * q + 4, :, :].bitcast(I32),
-                    xs_gathered[32 * q : 32 * q + 32, e * C : (e + 1) * C].bitcast(I32),
+                    x_planes[32 * q : 32 * q + 4, :, :].bitcast(I32),
+                    xs_gathered[16 * q : 16 * q + 16, :].bitcast(I32),
+                )
+
+        def move_last_pass_scales():
+            for q in QUADRANTS:
+                nc.sync.dma_start(
+                    x_last_plane[32 * q : 32 * q + 4, :].bitcast(I32),
+                    xs_gathered[64 + 4 * q : 64 + 4 * q + 4, :].bitcast(I32),
                 )
 
         def load_weights(e, lo, hi):
@@ -74,11 +79,14 @@ def tile_moe_nxt_lin_none_kernel(
             )
 
         w_planes = keep.tile([P, E * PASSES, N], U8, name="w_planes", align_bytes=64)
-        x_planes = [keep.tile([P, PLANES, C], U8, name=f"x_planes{e}", align_bytes=64) for e in range(E)]
+        x_planes = keep.tile([P, PASSES - 1, E * C], U8, name="x_planes", align_bytes=64)
+        x_last_plane = keep.tile([P, E * C], U8, name="x_last_plane", align_bytes=64)
         w_sb = [keep.tile([P, PASSES, 2 * N], U8, name=f"w_sb{e}", align_bytes=64) for e in range(E)]
         windows = [keep.tile([P, T], F32, name=f"window{u}") for u in range(2)]
         gate_rows = keep.tile([P, P], F32, name="gate_rows")
         zero_col = keep.tile([P, 1], F32, name="zero_col")
+        xs_window = keep.tile([P, T + SCALE_PAD], U8, name="xs_window")
+        nc.gpsimd.memset(xs_window[:].bitcast(I32), 0)
         nc.vector.memset(zero_col[:], 0.0)
         nc.vector.memset(gate_rows[:], 0.0)
         zero(w_planes[:, :PASSES, :], nc.vector)
@@ -86,13 +94,10 @@ def tile_moe_nxt_lin_none_kernel(
 
         offsets = keep.tile([P, SLOT_TILES * LIST_COLS], U16, name="offsets")
         nc.sync.dma_start(offsets[:], offs)
-        xs_window = keep.tile([P, T + SCALE_PAD], U8, name="xs_window")
-        nc.gpsimd.memset(xs_window[:, T:], 0)
-        for b in range(2):
-            nc.sync.dma_start(
-                xs_window[b:P:2, :T].bitcast(I32),
-                x_scales[b : b + PASSES - 1].rearrange("a q t -> q a t").bitcast(I32),
-            )
+        nc.sync.dma_start(
+            xs_window[:64, :T].bitcast(I32), x_scales[: PASSES - 1].rearrange("a q t -> q a t").bitcast(I32)
+        )
+        nc.sync.dma_start(xs_window[64:80, :T].bitcast(I32), x_scales[PASSES - 1].bitcast(I32))
         x_pass = []
         for lo, hi in ((0, X_FIRST), (X_FIRST, PASSES)):
             x_sb = keep.tile([P, hi - lo, T], U32, name=f"x_sb{lo}")
@@ -102,8 +107,9 @@ def tile_moe_nxt_lin_none_kernel(
         ident = keep.tile([P, P], F32, name="ident")
         make_identity(nc, ident[:])
         nc.sync.dma_start(gate_rows[:SLOT_TILES, :], gate[0].rearrange("(s p) -> s p", p=P))
-        zero(x_planes[0][:], nc.vector)
-        zero(x_planes[1][:], nc.gpsimd)
+        zero(x_planes[:, :2, :], nc.vector)
+        nc.vector.memset(x_last_plane[:].bitcast(I32), 0)
+        zero(x_planes[:, 2:, :], nc.gpsimd)
         for u in range(2):
             nc.scalar.copy(windows[u][:], zero_col[:].to_broadcast([P, T]))
         gate_turned = banks.tile([P, P], F32, name="gate_turned", tag="bank3")
@@ -114,10 +120,10 @@ def tile_moe_nxt_lin_none_kernel(
         xs_gathered = keep.tile([P, E * C], U8, name="xs_gathered", align_bytes=64)
         nc.vector.tensor_copy(xs_gathered[:], xs_window[:].indirect(offsets[:]))
         load_weights(0, 0, W_FIRST)
-        move_token_scales(0)
+        move_token_scales()
         load_weights(0, W_FIRST, PASSES)
+        move_last_pass_scales()
         load_weight_scales(1)
-        move_token_scales(1)
         load_weights(1, 0, W1_FIRST)
         load_weights(1, W1_FIRST, PASSES)
         wp_raw = keep.tile([P, PACK, M], F32, name="wp_raw")
@@ -157,7 +163,11 @@ def tile_moe_nxt_lin_none_kernel(
                 nc.tensor.matmul_mx(
                     out=y[:],
                     lhsT=x_gathered[e, a][:, h * P : (h + 1) * P].bitcast(FP8X4),
-                    lhsT_scale=x_planes[e][:, PLANE_OF_PASS[a], h * P : (h + 1) * P],
+                    lhsT_scale=(
+                        x_planes[:, a, s * P : (s + 1) * P]
+                        if a < PASSES - 1
+                        else x_last_plane[:, s * P : (s + 1) * P]
+                    ),
                     rhs=w_sb[e][:, a, :].bitcast(FP4X4),
                     rhs_scale=w_planes[:, e * PASSES + a, :],
                     start=(a == 0),
@@ -222,7 +232,10 @@ def tile_moe_nxt_lin_none_kernel(
             nc.vector.quantize_mx(out=codes[:].bitcast(FP8X4), scales=scales[:], in_=c_by_token[i][:])
             for f in range(FEATURE_TILES):
                 cols = slice(f * P, (f + 1) * P)
-                o = turned.tile([P, hi - lo], F32, name="o", tag="pairs")
+                if (i * FEATURE_TILES + f) % 8 < 4:
+                    o = banks.tile([P, hi - lo], F32, name="o", tag=f"bank{(i * FEATURE_TILES + f + 2) % 4}")
+                else:
+                    o = turned.tile([P, hi - lo], F32, name="o", tag="pairs")
                 nc.tensor.matmul_mx(
                     out=o[:],
                     lhsT=wp_codes[:, cols].bitcast(FP8X4),

@@ -28,9 +28,8 @@ LIST_COLS = P // 16
 
 X_FIRST = 2
 W_FIRST = 2
-W1_FIRST = 3
-WARM = ((1, 1, 8),)
-MID = 2
+WARM = 3
+XS_FIRST = P - 16 * PASSES
 VCOPY = ((2, 0), (2, 2))
 TOKEN_RUNS = ((0, 128), (128, 384), (384, 640))
 QUADRANTS = (0, 2, 1, 3)
@@ -52,107 +51,110 @@ def tile_moe_nxt_lin_none_kernel(
         def slot_offsets(lo, hi):
             return offsets[:, lo * LIST_COLS : hi * LIST_COLS]
 
-        def load_weight_scales(e):
-            for q in QUADRANTS:
-                nc.sync.dma_start(
-                    w_planes[32 * q : 32 * q + 4, e * PASSES : (e + 1) * PASSES, :].bitcast(I32),
-                    w_scales[e, :, 4 * q : 4 * q + 4, :].rearrange("a r n -> r a n").bitcast(I32),
+        def load_weight_scales(e, queue):
+            for r in range(4):
+                queue.dma_start(
+                    w_planes[e][r:P:32, :, :].bitcast(I32),
+                    w_scales[e, :, r:16:4, :].rearrange("a q n -> q a n").bitcast(I32),
                 )
 
         def move_token_scales():
             for q in QUADRANTS:
+                first = XS_FIRST + 16 + 16 * q
                 nc.sync.dma_start(
                     x_planes[32 * q : 32 * q + 4, :, :].bitcast(I32),
-                    xs_gathered[16 * q : 16 * q + 16, :].bitcast(I32),
+                    xs_gathered[first : first + 16, :].bitcast(I32),
                 )
 
         def move_last_pass_scales():
             for q in QUADRANTS:
+                first = XS_FIRST + 4 * q
                 nc.sync.dma_start(
                     x_last_plane[32 * q : 32 * q + 4, :].bitcast(I32),
-                    xs_gathered[64 + 4 * q : 64 + 4 * q + 4, :].bitcast(I32),
+                    xs_gathered[first : first + 4, :].bitcast(I32),
                 )
 
         def load_weights(e, lo, hi):
-            nc.sync.dma_start(
-                w_sb[e][:, lo:hi, :].bitcast(I32), w_words[e, lo:hi].rearrange("a p n -> p a n").bitcast(I32)
-            )
+            w_sb = keep.tile([P, hi - lo, 2 * N], U8, name=f"w_sb{e}_{lo}", align_bytes=64)
+            nc.sync.dma_start(w_sb[:].bitcast(I32), w_words[e, lo:hi].rearrange("a p n -> p a n").bitcast(I32))
+            w_pass[e].extend(w_sb[:, a, :] for a in range(hi - lo))
 
-        w_planes = keep.tile([P, E * PASSES, N], U8, name="w_planes", align_bytes=64)
+        w_planes = [keep.tile([P, PASSES, N], U8, name=f"w_planes{e}", align_bytes=64) for e in range(E)]
         x_planes = keep.tile([P, PASSES - 1, E * C], U8, name="x_planes", align_bytes=64)
         x_last_plane = keep.tile([P, E * C], U8, name="x_last_plane", align_bytes=64)
-        w_sb = [keep.tile([P, PASSES, 2 * N], U8, name=f"w_sb{e}", align_bytes=64) for e in range(E)]
+        w_pass = [[] for e in range(E)]
         windows = [keep.tile([P, T], F32, name=f"window{u}") for u in range(2)]
         gate_rows = keep.tile([P, P], F32, name="gate_rows")
         zero_col = keep.tile([P, 1], F32, name="zero_col")
         xs_window = keep.tile([P, T + SCALE_PAD], U8, name="xs_window")
-        nc.gpsimd.memset(xs_window[:].bitcast(I32), 0)
-        nc.vector.memset(zero_col[:], 0.0)
-        nc.vector.memset(gate_rows[:], 0.0)
-        zero(w_planes[:, :PASSES, :], nc.vector)
-        zero(w_planes[:, PASSES:, :], nc.gpsimd)
-
         offsets = keep.tile([P, SLOT_TILES * LIST_COLS], U16, name="offsets")
-        nc.sync.dma_start(offsets[:], offs)
         nc.sync.dma_start(
-            xs_window[:64, :T].bitcast(I32), x_scales[: PASSES - 1].rearrange("a q t -> q a t").bitcast(I32)
+            xs_window[XS_FIRST + 16 :, :T].bitcast(I32),
+            x_scales[: PASSES - 1].rearrange("a q t -> q a t").bitcast(I32),
         )
-        nc.sync.dma_start(xs_window[64:80, :T].bitcast(I32), x_scales[PASSES - 1].bitcast(I32))
+        nc.sync.dma_start(xs_window[XS_FIRST : XS_FIRST + 16, :T].bitcast(I32), x_scales[PASSES - 1].bitcast(I32))
+        nc.sync.dma_start(offsets[:], offs)
+        zero(w_planes[0][:], nc.vector)
+        nc.scalar.dma_start(gate_rows[P - SLOT_TILES :, :], gate[0].rearrange("(s p) -> s p", p=P))
+        nc.vector.memset(gate_rows[: P - SLOT_TILES, :], 0.0)
+        nc.vector.memset(zero_col[:], 0.0)
+        nc.vector.memset(xs_window[:XS_FIRST, :T].bitcast(I32), 0)
+        nc.vector.memset(xs_window[:, T:].bitcast(I32), 0)
+        zero(x_planes[:], nc.vector)
+        nc.vector.memset(x_last_plane[:].bitcast(I32), 0)
+        ident = keep.tile([P, P], F32, name="ident")
+        make_identity(nc, ident[:])
+        zero(w_planes[1][:], nc.gpsimd)
+        nc.scalar.copy(windows[0][:], zero_col[:].to_broadcast([P, T]))
+        nc.gpsimd.memset(windows[1][:], 0.0)
+
         x_pass = []
         for lo, hi in ((0, X_FIRST), (X_FIRST, PASSES)):
             x_sb = keep.tile([P, hi - lo, T], U32, name=f"x_sb{lo}")
             nc.sync.dma_start(x_sb[:].bitcast(I32), x_words[lo:hi].rearrange("a p t r -> p a (t r)").bitcast(I32))
             x_pass.extend(x_sb[:, a, :] for a in range(hi - lo))
-        load_weight_scales(0)
-        ident = keep.tile([P, P], F32, name="ident")
-        make_identity(nc, ident[:])
-        nc.sync.dma_start(gate_rows[:SLOT_TILES, :], gate[0].rearrange("(s p) -> s p", p=P))
-        zero(x_planes[:, :2, :], nc.vector)
-        nc.vector.memset(x_last_plane[:].bitcast(I32), 0)
-        zero(x_planes[:, 2:, :], nc.gpsimd)
-        for u in range(2):
-            nc.scalar.copy(windows[u][:], zero_col[:].to_broadcast([P, T]))
-        gate_turned = banks.tile([P, P], F32, name="gate_turned", tag="bank3")
-        nc.tensor.transpose(gate_turned[:], gate_rows[:], ident[:])
-        gate_col = keep.tile([P, SLOT_TILES], F32, name="gate_col")
-        nc.scalar.copy(gate_col[:], gate_turned[:, :SLOT_TILES])
+            if lo == 0:
+                load_weight_scales(0, nc.sync)
 
         xs_gathered = keep.tile([P, E * C], U8, name="xs_gathered", align_bytes=64)
         nc.vector.tensor_copy(xs_gathered[:], xs_window[:].indirect(offsets[:]))
+        gate_turned = banks.tile([P, P], F32, name="gate_turned", tag="bank3")
+        nc.tensor.transpose(gate_turned[:], gate_rows[:], ident[:])
+        gate_col = keep.tile([P, SLOT_TILES], F32, name="gate_col")
+        nc.scalar.copy(gate_col[:], gate_turned[:, P - SLOT_TILES :])
         load_weights(0, 0, W_FIRST)
         move_token_scales()
         load_weights(0, W_FIRST, PASSES)
         move_last_pass_scales()
-        load_weight_scales(1)
-        load_weights(1, 0, W1_FIRST)
-        load_weights(1, W1_FIRST, PASSES)
+        load_weights(1, 0, PASSES)
+        load_weight_scales(1, nc.sync)
         wp_raw = keep.tile([P, PACK, M], F32, name="wp_raw")
         nc.sync.dma_start(wp_raw[:], wp.rearrange("(p j) f -> p j f", j=PACK))
 
-        x_gathered = {}
-        for lo, hi in ((0, X_FIRST), (X_FIRST, PASSES)):
+        x_gathered = [keep.tile([P, E * C], U32, name=f"x_gathered{a}", align_bytes=64) for a in range(PASSES)]
+
+        def gather_words(e, a):
+            slots = slot_offsets(e * TILES_PER_EXPERT, (e + 1) * TILES_PER_EXPERT)
+            nc.vector.tensor_copy(x_gathered[a][:, e * C : (e + 1) * C], x_pass[a].indirect(slots))
+
+        for a in range(X_FIRST):
             for e in range(E):
-                for a in range(lo, hi):
-                    words = keep.tile([P, C], U32, name=f"x_gathered{e}_{a}", align_bytes=64)
-                    slots = slot_offsets(e * TILES_PER_EXPERT, (e + 1) * TILES_PER_EXPERT)
-                    nc.vector.tensor_copy(words[:], x_pass[a].indirect(slots))
-                    x_gathered[e, a] = words
+                gather_words(e, a)
+        for e in range(E):
+            for a in range(X_FIRST, PASSES):
+                gather_words(e, a)
 
-        def warm_up(words, passes, bank):
-            warm = banks.tile([P, C], F32, name="warm", tag=bank)
-            for i in range(passes):
-                nc.tensor.matmul_mx(
-                    out=warm[:],
-                    lhsT=words[:, :P].bitcast(FP8X4),
-                    lhsT_scale=xs_gathered[:, :P],
-                    rhs=words[:].bitcast(FP8X4),
-                    rhs_scale=xs_gathered[:, :C],
-                    start=True,
-                    stop=True,
-                )
-
-        for e, a, passes in WARM:
-            warm_up(x_gathered[e, a], passes, "bank2")
+        warm = banks.tile([P, N], F32, name="warm", tag="bank2")
+        for i in range(WARM):
+            nc.tensor.matmul_mx(
+                out=warm[:],
+                lhsT=x_gathered[0][:, :P].bitcast(FP8X4),
+                lhsT_scale=xs_gathered[:, :P],
+                rhs=x_gathered[0][:].bitcast(FP8X4),
+                rhs_scale=xs_gathered[:],
+                start=True,
+                stop=True,
+            )
 
         c_pairs = {(s, u): keep.tile([P, P], F32, name=f"c_pairs{s}_{u}") for s in range(SLOT_TILES) for u in range(2)}
 
@@ -162,21 +164,17 @@ def tile_moe_nxt_lin_none_kernel(
             for a in range(PASSES):
                 nc.tensor.matmul_mx(
                     out=y[:],
-                    lhsT=x_gathered[e, a][:, h * P : (h + 1) * P].bitcast(FP8X4),
-                    lhsT_scale=(
-                        x_planes[:, a, s * P : (s + 1) * P]
-                        if a < PASSES - 1
-                        else x_last_plane[:, s * P : (s + 1) * P]
-                    ),
-                    rhs=w_sb[e][:, a, :].bitcast(FP4X4),
-                    rhs_scale=w_planes[:, e * PASSES + a, :],
+                    lhsT=x_gathered[a][:, s * P : (s + 1) * P].bitcast(FP8X4),
+                    lhsT_scale=(x_planes[:, a, :] if a < PASSES - 1 else x_last_plane[:])[:, s * P : (s + 1) * P],
+                    rhs=w_pass[e][a].bitcast(FP4X4),
+                    rhs_scale=w_planes[e][:, a, :],
                     start=(a == 0),
                     stop=(a == PASSES - 1),
                 )
             y_by_u = y[:].rearrange("s (p u d) -> s u p d", u=2, d=2)
             halves = []
             for u in range(2):
-                half = keep.tile([P, 2 * P], BF16, name=f"c_by_slot{s}_{u}", tag=f"stage{s}_{u}", align_bytes=64)
+                half = keep.tile([P, 2 * P], BF16, name=f"c_by_slot{s}_{u}", align_bytes=64)
                 nc.scalar.activation(
                     half[:].rearrange("s (p d) -> s p d", d=2), y_by_u[:, u], COPY, scale=gate_col[:, s : s + 1]
                 )
@@ -197,8 +195,11 @@ def tile_moe_nxt_lin_none_kernel(
 
         def quantise_wp(lo, hi):
             cols = slice(lo * P, hi * P)
-            wp_bf = keep.tile([P, (hi - lo) * P, PACK], BF16, name=f"wp_bf{lo}", tag=f"stage{lo + 1}_1", align_bytes=64)
-            nc.scalar.copy(wp_bf[:], wp_raw[:, :, cols].rearrange("p j f -> p f j"))
+            wp_bf = keep.tile([P, (hi - lo) * P, PACK], BF16, name=f"wp_bf{lo}", align_bytes=64)
+            nc.scalar.copy(
+                wp_bf[:].rearrange("p (c i) j -> p c j i", i=4),
+                wp_raw[:, :, cols].rearrange("p j (c i) -> p c j i", i=4),
+            )
             nc.vector.quantize_mx(
                 out=wp_codes[:, cols].bitcast(FP8X4),
                 scales=wp_scales[:, cols],
@@ -209,8 +210,6 @@ def tile_moe_nxt_lin_none_kernel(
             gated_expert(s)
             scatter(0, s, s + 1)
             scatter(1, s, s + 1)
-            if s == 1 and MID:
-                warm_up(x_gathered[0, 0], MID, "bank0")
         for f in range(FEATURE_TILES):
             quantise_wp(f, f + 1)
 

@@ -28,7 +28,7 @@ LIST_COLS = P // 16
 
 X_FIRST = 2
 W_FIRST = 2
-WARM = 3
+W1_FIRST = 3
 XS_FIRST = P - 16 * PASSES
 VCOPY = ((2, 0), (2, 2))
 TOKEN_RUNS = ((0, 128), (128, 384), (384, 640))
@@ -96,12 +96,13 @@ def tile_moe_nxt_lin_none_kernel(
         nc.sync.dma_start(offsets[:], offs)
         zero(w_planes[0][:], nc.vector)
         nc.scalar.dma_start(gate_rows[P - SLOT_TILES :, :], gate[0].rearrange("(s p) -> s p", p=P))
+        load_weight_scales(0, nc.scalar)
         nc.vector.memset(gate_rows[: P - SLOT_TILES, :], 0.0)
-        nc.vector.memset(zero_col[:], 0.0)
         nc.vector.memset(xs_window[:XS_FIRST, :T].bitcast(I32), 0)
         nc.vector.memset(xs_window[:, T:].bitcast(I32), 0)
         zero(x_planes[:], nc.vector)
         nc.vector.memset(x_last_plane[:].bitcast(I32), 0)
+        nc.vector.memset(zero_col[:], 0.0)
         ident = keep.tile([P, P], F32, name="ident")
         make_identity(nc, ident[:])
         zero(w_planes[1][:], nc.gpsimd)
@@ -113,8 +114,6 @@ def tile_moe_nxt_lin_none_kernel(
             x_sb = keep.tile([P, hi - lo, T], U32, name=f"x_sb{lo}")
             nc.sync.dma_start(x_sb[:].bitcast(I32), x_words[lo:hi].rearrange("a p t r -> p a (t r)").bitcast(I32))
             x_pass.extend(x_sb[:, a, :] for a in range(hi - lo))
-            if lo == 0:
-                load_weight_scales(0, nc.sync)
 
         xs_gathered = keep.tile([P, E * C], U8, name="xs_gathered", align_bytes=64)
         nc.vector.tensor_copy(xs_gathered[:], xs_window[:].indirect(offsets[:]))
@@ -126,8 +125,9 @@ def tile_moe_nxt_lin_none_kernel(
         move_token_scales()
         load_weights(0, W_FIRST, PASSES)
         move_last_pass_scales()
-        load_weights(1, 0, PASSES)
         load_weight_scales(1, nc.sync)
+        load_weights(1, 0, W1_FIRST)
+        load_weights(1, W1_FIRST, PASSES)
         wp_raw = keep.tile([P, PACK, M], F32, name="wp_raw")
         nc.sync.dma_start(wp_raw[:], wp.rearrange("(p j) f -> p j f", j=PACK))
 
@@ -143,18 +143,6 @@ def tile_moe_nxt_lin_none_kernel(
         for e in range(E):
             for a in range(X_FIRST, PASSES):
                 gather_words(e, a)
-
-        warm = banks.tile([P, N], F32, name="warm", tag="bank2")
-        for i in range(WARM):
-            nc.tensor.matmul_mx(
-                out=warm[:],
-                lhsT=x_gathered[0][:, :P].bitcast(FP8X4),
-                lhsT_scale=xs_gathered[:, :P],
-                rhs=x_gathered[0][:].bitcast(FP8X4),
-                rhs_scale=xs_gathered[:],
-                start=True,
-                stop=True,
-            )
 
         c_pairs = {(s, u): keep.tile([P, P], F32, name=f"c_pairs{s}_{u}") for s in range(SLOT_TILES) for u in range(2)}
 
@@ -196,10 +184,7 @@ def tile_moe_nxt_lin_none_kernel(
         def quantise_wp(lo, hi):
             cols = slice(lo * P, hi * P)
             wp_bf = keep.tile([P, (hi - lo) * P, PACK], BF16, name=f"wp_bf{lo}", align_bytes=64)
-            nc.scalar.copy(
-                wp_bf[:].rearrange("p (c i) j -> p c j i", i=4),
-                wp_raw[:, :, cols].rearrange("p j (c i) -> p c j i", i=4),
-            )
+            nc.scalar.copy(wp_bf[:], wp_raw[:, :, cols].rearrange("p j f -> p f j"))
             nc.vector.quantize_mx(
                 out=wp_codes[:, cols].bitcast(FP8X4),
                 scales=wp_scales[:, cols],

@@ -29,6 +29,7 @@ LIST_COLS = P // 16
 X_FIRST = 2
 W_FIRST = 2
 W1_FIRST = 3
+WARM = 3
 XS_FIRST = P - 16 * PASSES
 VCOPY = ((2, 0), (2, 2))
 TOKEN_RUNS = ((0, 128), (128, 384), (384, 640))
@@ -143,6 +144,18 @@ def tile_moe_nxt_lin_none_kernel(
         for e in range(E):
             for a in range(X_FIRST, PASSES):
                 gather_words(e, a)
+
+        warm = banks.tile([P, N], F32, name="warm", tag="bank2")
+        for i in range(WARM):
+            nc.tensor.matmul_mx(
+                out=warm[:],
+                lhsT=x_gathered[X_FIRST - 1][:, :P].bitcast(FP8X4),
+                lhsT_scale=xs_gathered[:, :P],
+                rhs=x_gathered[X_FIRST - 1][:].bitcast(FP8X4),
+                rhs_scale=xs_gathered[:],
+                start=True,
+                stop=True,
+            )
 
         c_pairs = {(s, u): keep.tile([P, P], F32, name=f"c_pairs{s}_{u}") for s in range(SLOT_TILES) for u in range(2)}
 

@@ -28,8 +28,9 @@ LIST_COLS = P // 16
 
 X_FIRST = 2
 W_FIRST = 2
-W1_FIRST = 3
+W1_FIRST = 2
 WARM = 3
+DOUBLED = ((0, 384), (384, 640))
 XS_FIRST = P - 16 * PASSES
 VCOPY = ((2, 0), (2, 2))
 TOKEN_RUNS = ((0, 128), (128, 384), (384, 640))
@@ -93,11 +94,10 @@ def tile_moe_nxt_lin_none_kernel(
             xs_window[XS_FIRST + 16 :, :T].bitcast(I32),
             x_scales[: PASSES - 1].rearrange("a q t -> q a t").bitcast(I32),
         )
-        nc.sync.dma_start(xs_window[XS_FIRST : XS_FIRST + 16, :T].bitcast(I32), x_scales[PASSES - 1].bitcast(I32))
         nc.sync.dma_start(offsets[:], offs)
+        nc.scalar.dma_start(xs_window[XS_FIRST : XS_FIRST + 16, :T].bitcast(I32), x_scales[PASSES - 1].bitcast(I32))
         zero(w_planes[0][:], nc.vector)
         nc.scalar.dma_start(gate_rows[P - SLOT_TILES :, :], gate[0].rearrange("(s p) -> s p", p=P))
-        load_weight_scales(0, nc.scalar)
         nc.vector.memset(gate_rows[: P - SLOT_TILES, :], 0.0)
         nc.vector.memset(xs_window[:XS_FIRST, :T].bitcast(I32), 0)
         nc.vector.memset(xs_window[:, T:].bitcast(I32), 0)
@@ -112,9 +112,16 @@ def tile_moe_nxt_lin_none_kernel(
 
         x_pass = []
         for lo, hi in ((0, X_FIRST), (X_FIRST, PASSES)):
-            x_sb = keep.tile([P, hi - lo, T], U32, name=f"x_sb{lo}")
-            nc.sync.dma_start(x_sb[:].bitcast(I32), x_words[lo:hi].rearrange("a p t r -> p a (t r)").bitcast(I32))
-            x_pass.extend(x_sb[:, a, :] for a in range(hi - lo))
+            pad = SCALE_PAD if lo == 0 else 0
+            x_sb = keep.tile([P, (hi - lo) * T + pad], U32, name=f"x_sb{lo}")
+            nc.sync.dma_start(
+                x_sb[:, : (hi - lo) * T].bitcast(I32).rearrange("p (a t) -> p a t", t=T),
+                x_words[lo:hi].rearrange("a p t r -> p a (t r)").bitcast(I32),
+            )
+            if pad:
+                nc.vector.memset(x_sb[:, (hi - lo) * T :].bitcast(I32), 0)
+                load_weight_scales(0, nc.sync)
+            x_pass.extend(x_sb[:, a * T : (a + 1) * T + pad] for a in range(hi - lo))
 
         xs_gathered = keep.tile([P, E * C], U8, name="xs_gathered", align_bytes=64)
         nc.vector.tensor_copy(xs_gathered[:], xs_window[:].indirect(offsets[:]))
@@ -139,8 +146,7 @@ def tile_moe_nxt_lin_none_kernel(
             nc.vector.tensor_copy(x_gathered[a][:, e * C : (e + 1) * C], x_pass[a].indirect(slots))
 
         for a in range(X_FIRST):
-            for e in range(E):
-                gather_words(e, a)
+            nc.vector.tensor_copy(x_gathered[a][:], x_pass[a].indirect(offsets[:]))
         for e in range(E):
             for a in range(X_FIRST, PASSES):
                 gather_words(e, a)
@@ -149,9 +155,9 @@ def tile_moe_nxt_lin_none_kernel(
         for i in range(WARM):
             nc.tensor.matmul_mx(
                 out=warm[:],
-                lhsT=x_gathered[X_FIRST - 1][:, :P].bitcast(FP8X4),
+                lhsT=x_gathered[0][:, :P].bitcast(FP8X4),
                 lhsT_scale=xs_gathered[:, :P],
-                rhs=x_gathered[X_FIRST - 1][:].bitcast(FP8X4),
+                rhs=x_gathered[0][:].bitcast(FP8X4),
                 rhs_scale=xs_gathered[:],
                 start=True,
                 stop=True,
@@ -211,12 +217,12 @@ def tile_moe_nxt_lin_none_kernel(
         for f in range(FEATURE_TILES):
             quantise_wp(f, f + 1)
 
-        c_by_token = [
-            keep.tile([P, (hi - lo) * PACK], BF16, name=f"c_by_token{lo}", align_bytes=64) for lo, hi in TOKEN_RUNS
-        ]
-        c_words = [c[:].bitcast(F32).rearrange("p (t u) -> p t u", u=2) for c in c_by_token]
-        for words, (lo, hi) in zip(c_words, TOKEN_RUNS):
-            nc.scalar.copy(words, windows[0][:, lo:hi].unsqueeze(2).to_broadcast([P, hi - lo, 2]))
+        c_all = keep.tile([P, T * PACK], BF16, name="c_all", align_bytes=64)
+        c_by_token = [c_all[:, lo * PACK : hi * PACK] for lo, hi in TOKEN_RUNS]
+        words = c_all[:].bitcast(F32).rearrange("p (t u) -> p t u", u=2)
+        c_words = [words[:, lo:hi, :] for lo, hi in TOKEN_RUNS]
+        for lo, hi in DOUBLED:
+            nc.scalar.copy(words[:, lo:hi, :], windows[0][:, lo:hi].unsqueeze(2).to_broadcast([P, hi - lo, 2]))
 
         def weave(i):
             lo, hi = TOKEN_RUNS[i]
@@ -226,7 +232,7 @@ def tile_moe_nxt_lin_none_kernel(
             lo, hi = TOKEN_RUNS[i]
             codes = keep.tile([P, hi - lo], U32, name=f"c_codes{i}", align_bytes=64)
             scales = keep.tile([P, hi - lo], U8, name=f"c_scales{i}", align_bytes=64)
-            nc.vector.quantize_mx(out=codes[:].bitcast(FP8X4), scales=scales[:], in_=c_by_token[i][:])
+            nc.vector.quantize_mx(out=codes[:].bitcast(FP8X4), scales=scales[:], in_=c_by_token[i])
             for f in range(FEATURE_TILES):
                 cols = slice(f * P, (f + 1) * P)
                 if (i * FEATURE_TILES + f) % 8 < 4:

@@ -28,8 +28,9 @@ LIST_COLS = P // 16
 
 X_FIRST = 2
 W_FIRST = 2
-W1_FIRST = 2
+W1_FIRST = 3
 WARM = 3
+STORE_GROUPS = (((0,), (1, 2)), ((0,), (1,), (2,)), ((0,), (1,), (2,)))
 DOUBLED = ((0, 384), (384, 640))
 XS_FIRST = P - 16 * PASSES
 VCOPY = ((2, 0), (2, 2))
@@ -98,6 +99,7 @@ def tile_moe_nxt_lin_none_kernel(
         nc.scalar.dma_start(xs_window[XS_FIRST : XS_FIRST + 16, :T].bitcast(I32), x_scales[PASSES - 1].bitcast(I32))
         zero(w_planes[0][:], nc.vector)
         nc.scalar.dma_start(gate_rows[P - SLOT_TILES :, :], gate[0].rearrange("(s p) -> s p", p=P))
+        load_weight_scales(0, nc.scalar)
         nc.vector.memset(gate_rows[: P - SLOT_TILES, :], 0.0)
         nc.vector.memset(xs_window[:XS_FIRST, :T].bitcast(I32), 0)
         nc.vector.memset(xs_window[:, T:].bitcast(I32), 0)
@@ -106,9 +108,9 @@ def tile_moe_nxt_lin_none_kernel(
         nc.vector.memset(zero_col[:], 0.0)
         ident = keep.tile([P, P], F32, name="ident")
         make_identity(nc, ident[:])
-        zero(w_planes[1][:], nc.gpsimd)
-        nc.scalar.copy(windows[0][:], zero_col[:].to_broadcast([P, T]))
-        nc.gpsimd.memset(windows[1][:], 0.0)
+        zero(w_planes[1][:], nc.vector)
+        for window in windows:
+            nc.scalar.copy(window[:], zero_col[:].to_broadcast([P, T]))
 
         x_pass = []
         for lo, hi in ((0, X_FIRST), (X_FIRST, PASSES)):
@@ -120,7 +122,6 @@ def tile_moe_nxt_lin_none_kernel(
             )
             if pad:
                 nc.vector.memset(x_sb[:, (hi - lo) * T :].bitcast(I32), 0)
-                load_weight_scales(0, nc.sync)
             x_pass.extend(x_sb[:, a * T : (a + 1) * T + pad] for a in range(hi - lo))
 
         xs_gathered = keep.tile([P, E * C], U8, name="xs_gathered", align_bytes=64)
@@ -155,9 +156,9 @@ def tile_moe_nxt_lin_none_kernel(
         for i in range(WARM):
             nc.tensor.matmul_mx(
                 out=warm[:],
-                lhsT=x_gathered[0][:, :P].bitcast(FP8X4),
+                lhsT=x_gathered[X_FIRST - 1][:, :P].bitcast(FP8X4),
                 lhsT_scale=xs_gathered[:, :P],
-                rhs=x_gathered[0][:].bitcast(FP8X4),
+                rhs=x_gathered[X_FIRST - 1][:].bitcast(FP8X4),
                 rhs_scale=xs_gathered[:],
                 start=True,
                 stop=True,
@@ -168,23 +169,28 @@ def tile_moe_nxt_lin_none_kernel(
         def gated_expert(s):
             e, h = divmod(s, TILES_PER_EXPERT)
             y = banks.tile([P, N], F32, name="y", tag=f"bank{h}")
-            for a in range(PASSES):
+            order = list(range(PASSES))
+            if s == SLOT_TILES - 1:
+                order = order[-1:] + order[:-1]
+            for a in order:
                 nc.tensor.matmul_mx(
                     out=y[:],
                     lhsT=x_gathered[a][:, s * P : (s + 1) * P].bitcast(FP8X4),
                     lhsT_scale=(x_planes[:, a, :] if a < PASSES - 1 else x_last_plane[:])[:, s * P : (s + 1) * P],
                     rhs=w_pass[e][a].bitcast(FP4X4),
                     rhs_scale=w_planes[e][:, a, :],
-                    start=(a == 0),
-                    stop=(a == PASSES - 1),
+                    start=(a == order[0]),
+                    stop=(a == order[-1]),
                 )
             y_by_u = y[:].rearrange("s (p u d) -> s u p d", u=2, d=2)
             halves = []
             for u in range(2):
                 half = keep.tile([P, 2 * P], BF16, name=f"c_by_slot{s}_{u}", align_bytes=64)
-                nc.scalar.activation(
-                    half[:].rearrange("s (p d) -> s p d", d=2), y_by_u[:, u], COPY, scale=gate_col[:, s : s + 1]
-                )
+                rounded = half[:].rearrange("s (p d) -> s p d", d=2)
+                if s == 1:
+                    nc.vector.tensor_scalar(rounded, y_by_u[:, u], gate_col[:, s : s + 1], None, mybir.AluOpType.mult)
+                else:
+                    nc.scalar.activation(rounded, y_by_u[:, u], COPY, scale=gate_col[:, s : s + 1])
                 halves.append(half)
             for u in range(2):
                 pairs = turned.tile([P, P], F32, name="pairs", tag="pairs")
@@ -233,25 +239,31 @@ def tile_moe_nxt_lin_none_kernel(
             codes = keep.tile([P, hi - lo], U32, name=f"c_codes{i}", align_bytes=64)
             scales = keep.tile([P, hi - lo], U8, name=f"c_scales{i}", align_bytes=64)
             nc.vector.quantize_mx(out=codes[:].bitcast(FP8X4), scales=scales[:], in_=c_by_token[i])
-            for f in range(FEATURE_TILES):
-                cols = slice(f * P, (f + 1) * P)
-                if (i * FEATURE_TILES + f) % 8 < 4:
-                    o = banks.tile([P, hi - lo], F32, name="o", tag=f"bank{(i * FEATURE_TILES + f + 2) % 4}")
+            for group in STORE_GROUPS[i]:
+                n = len(stored)
+                stored.append(group)
+                shape = [P, len(group), hi - lo]
+                if n < 4:
+                    o = banks.tile(shape, F32, name="o", tag=f"bank{(n + 2) % 4}")
                 else:
-                    o = turned.tile([P, hi - lo], F32, name="o", tag="pairs")
-                nc.tensor.matmul_mx(
-                    out=o[:],
-                    lhsT=wp_codes[:, cols].bitcast(FP8X4),
-                    lhsT_scale=wp_scales[:, cols],
-                    rhs=codes[:].bitcast(FP8X4),
-                    rhs_scale=scales[:],
-                    start=True,
-                    stop=True,
-                )
-                o_sb = keep.tile([P, hi - lo], F32, name=f"o_sb{i}_{f}")
-                (nc.vector.tensor_copy if (i, f) in VCOPY else nc.scalar.copy)(o_sb[:], o[:])
-                nc.sync.dma_start(out[cols, lo:hi], o_sb[:])
+                    o = turned.tile(shape, F32, name="o", tag="pairs")
+                for j, f in enumerate(group):
+                    cols = slice(f * P, (f + 1) * P)
+                    nc.tensor.matmul_mx(
+                        out=o[:, j, :],
+                        lhsT=wp_codes[:, cols].bitcast(FP8X4),
+                        lhsT_scale=wp_scales[:, cols],
+                        rhs=codes[:].bitcast(FP8X4),
+                        rhs_scale=scales[:],
+                        start=True,
+                        stop=True,
+                    )
+                o_sb = keep.tile(shape, F32, name=f"o_sb{n}")
+                (nc.vector.tensor_copy if (i, group[0]) in VCOPY else nc.scalar.copy)(o_sb[:], o[:])
+                rows = out[group[0] * P : (group[-1] + 1) * P, lo:hi]
+                nc.sync.dma_start(rows.rearrange("(f p) t -> p f t", p=P), o_sb[:])
 
+        stored = []
         weave(0)
         for i in range(len(TOKEN_RUNS)):
             if i + 1 < len(TOKEN_RUNS):

@@ -27,7 +27,7 @@ BANKS = 6
 LIST_COLS = P // 16
 
 X_FIRST = 2
-W_FIRST = 2
+W_FIRST = 3
 W1_FIRST = 3
 WARM = 3
 STORE_GROUPS = (((0,), (1, 2)), ((0,), (1,), (2,)), ((0,), (1,), (2,)))
@@ -113,7 +113,8 @@ def tile_moe_nxt_lin_none_kernel(
             nc.scalar.copy(window[:], zero_col[:].to_broadcast([P, T]))
 
         x_pass = []
-        for lo, hi in ((0, X_FIRST), (X_FIRST, PASSES)):
+
+        def load_tokens(lo, hi):
             pad = SCALE_PAD if lo == 0 else 0
             x_sb = keep.tile([P, (hi - lo) * T + pad], U32, name=f"x_sb{lo}")
             nc.sync.dma_start(
@@ -124,6 +125,9 @@ def tile_moe_nxt_lin_none_kernel(
                 nc.vector.memset(x_sb[:, (hi - lo) * T :].bitcast(I32), 0)
             x_pass.extend(x_sb[:, a * T : (a + 1) * T + pad] for a in range(hi - lo))
 
+        load_tokens(0, X_FIRST)
+        load_tokens(X_FIRST, W_FIRST)
+
         xs_gathered = keep.tile([P, E * C], U8, name="xs_gathered", align_bytes=64)
         nc.vector.tensor_copy(xs_gathered[:], xs_window[:].indirect(offsets[:]))
         gate_turned = banks.tile([P, P], F32, name="gate_turned", tag="bank3")
@@ -132,6 +136,7 @@ def tile_moe_nxt_lin_none_kernel(
         nc.scalar.copy(gate_col[:], gate_turned[:, P - SLOT_TILES :])
         load_weights(0, 0, W_FIRST)
         move_token_scales()
+        load_tokens(W_FIRST, PASSES)
         load_weights(0, W_FIRST, PASSES)
         move_last_pass_scales()
         load_weight_scales(1, nc.sync)
@@ -148,9 +153,10 @@ def tile_moe_nxt_lin_none_kernel(
 
         for a in range(X_FIRST):
             nc.vector.tensor_copy(x_gathered[a][:], x_pass[a].indirect(offsets[:]))
-        for e in range(E):
-            for a in range(X_FIRST, PASSES):
-                gather_words(e, a)
+        for lo, hi in ((X_FIRST, W_FIRST), (W_FIRST, PASSES)):
+            for e in range(E):
+                for a in range(lo, hi):
+                    gather_words(e, a)
 
         warm = banks.tile([P, N], F32, name="warm", tag="bank2")
         for i in range(WARM):

@@ -115,15 +115,14 @@ def tile_moe_nxt_lin_none_kernel(
         x_pass = []
 
         def load_tokens(lo, hi):
-            pad = SCALE_PAD if lo == 0 else 0
-            x_sb = keep.tile([P, (hi - lo) * T + pad], U32, name=f"x_sb{lo}")
+            x_sb = keep.tile([P, (hi - lo) * T], U32, name=f"x_sb{lo}")
             nc.sync.dma_start(
-                x_sb[:, : (hi - lo) * T].bitcast(I32).rearrange("p (a t) -> p a t", t=T),
+                x_sb[:].bitcast(I32).rearrange("p (a t) -> p a t", t=T),
                 x_words[lo:hi].rearrange("a p t r -> p a (t r)").bitcast(I32),
             )
-            if pad:
-                nc.vector.memset(x_sb[:, (hi - lo) * T :].bitcast(I32), 0)
-            x_pass.extend(x_sb[:, a * T : (a + 1) * T + pad] for a in range(hi - lo))
+            for a in range(lo, hi):
+                over = SCALE_PAD if a == 0 else 0
+                x_pass.append(x_sb[:, (a - lo) * T : (a - lo + 1) * T + over])
 
         load_tokens(0, X_FIRST)
         load_tokens(X_FIRST, W_FIRST)
@@ -139,8 +138,8 @@ def tile_moe_nxt_lin_none_kernel(
         load_tokens(W_FIRST, PASSES)
         load_weights(0, W_FIRST, PASSES)
         move_last_pass_scales()
-        load_weight_scales(1, nc.sync)
         load_weights(1, 0, W1_FIRST)
+        load_weight_scales(1, nc.sync)
         load_weights(1, W1_FIRST, PASSES)
         wp_raw = keep.tile([P, PACK, M], F32, name="wp_raw")
         nc.sync.dma_start(wp_raw[:], wp.rearrange("(p j) f -> p j f", j=PACK))
@@ -151,8 +150,9 @@ def tile_moe_nxt_lin_none_kernel(
             slots = slot_offsets(e * TILES_PER_EXPERT, (e + 1) * TILES_PER_EXPERT)
             nc.vector.tensor_copy(x_gathered[a][:, e * C : (e + 1) * C], x_pass[a].indirect(slots))
 
-        for a in range(X_FIRST):
-            nc.vector.tensor_copy(x_gathered[a][:], x_pass[a].indirect(offsets[:]))
+        nc.vector.tensor_copy(x_gathered[0][:], x_pass[0].indirect(offsets[:]))
+        for e in range(E):
+            gather_words(e, 1)
         for lo, hi in ((X_FIRST, W_FIRST), (W_FIRST, PASSES)):
             for e in range(E):
                 for a in range(lo, hi):
@@ -164,7 +164,7 @@ def tile_moe_nxt_lin_none_kernel(
                 out=warm[:],
                 lhsT=x_gathered[X_FIRST - 1][:, :P].bitcast(FP8X4),
                 lhsT_scale=xs_gathered[:, :P],
-                rhs=x_gathered[X_FIRST - 1][:].bitcast(FP8X4),
+                rhs=x_gathered[0][:].bitcast(FP8X4),
                 rhs_scale=xs_gathered[:],
                 start=True,
                 stop=True,

@@ -170,7 +170,7 @@ def tile_moe_nxt_lin_none_kernel(
                 stop=True,
             )
 
-        c_pairs = {(s, u): keep.tile([P, P], F32, name=f"c_pairs{s}_{u}") for s in range(SLOT_TILES) for u in range(2)}
+        c_pairs = {(s, u): keep.tile([P, P], F32, name=f"c_pairs{s}_{u}", tag=f"last{u}" if s == SLOT_TILES - 1 else f"pairs{s}_{u}", align_bytes=64) for s in range(SLOT_TILES) for u in range(2)}
 
         def gated_expert(s):
             e, h = divmod(s, TILES_PER_EXPERT)
@@ -209,15 +209,16 @@ def tile_moe_nxt_lin_none_kernel(
                 windows[u][:].indirect(slot_offsets(lo, hi)), c_pairs[lo, u][:]
             )
 
-        wp_codes = keep.tile([P, M], U32, name="wp_codes", align_bytes=64)
+        wp_codes = {}
         wp_scales = keep.tile([P, M], U8, name="wp_scales", align_bytes=64)
 
         def quantise_wp(lo, hi):
             cols = slice(lo * P, hi * P)
             wp_bf = keep.tile([P, (hi - lo) * P, PACK], BF16, name=f"wp_bf{lo}", align_bytes=64)
             nc.scalar.copy(wp_bf[:], wp_raw[:, :, cols].rearrange("p j f -> p f j"))
+            wp_codes[lo] = keep.tile([P, P], U32, name=f"wp_codes{lo}", tag=("wp0", "last1", "last0")[lo], align_bytes=64)
             nc.vector.quantize_mx(
-                out=wp_codes[:, cols].bitcast(FP8X4),
+                out=wp_codes[lo][:].bitcast(FP8X4),
                 scales=wp_scales[:, cols],
                 in_=wp_bf[:].rearrange("p f j -> p (f j)"),
             )
@@ -257,7 +258,7 @@ def tile_moe_nxt_lin_none_kernel(
                     cols = slice(f * P, (f + 1) * P)
                     nc.tensor.matmul_mx(
                         out=o[:, j, :],
-                        lhsT=wp_codes[:, cols].bitcast(FP8X4),
+                        lhsT=wp_codes[f][:].bitcast(FP8X4),
                         lhsT_scale=wp_scales[:, cols],
                         rhs=codes[:].bitcast(FP8X4),
                         rhs_scale=scales[:],

@@ -29,7 +29,7 @@ LIST_COLS = P // 16
 X_FIRST = 2
 W_FIRST = 3
 W1_FIRST = 3
-WARM = 3
+WARM = 2
 STORE_GROUPS = (((0,), (1, 2)), ((0,), (1,), (2,)), ((0,), (1,), (2,)))
 DOUBLED = ((0, 384), (384, 640))
 XS_FIRST = P - 16 * PASSES
@@ -70,11 +70,10 @@ def tile_moe_nxt_lin_none_kernel(
                 )
 
         def move_last_pass_scales():
-            for q in QUADRANTS:
-                first = XS_FIRST + 4 * q
+            for r in range(4):
                 nc.sync.dma_start(
-                    x_last_plane[32 * q : 32 * q + 4, :].bitcast(I32),
-                    xs_gathered[first : first + 4, :].bitcast(I32),
+                    x_last_plane[r:P:32, :].bitcast(I32),
+                    xs_gathered[XS_FIRST + r : XS_FIRST + 16 : 4, :].bitcast(I32),
                 )
 
         def load_weights(e, lo, hi):

@@ -171,15 +171,19 @@ def tile_moe_nxt_lin_none_kernel(
 
         c_pairs = {(s, u): keep.tile([P, P], F32, name=f"c_pairs{s}_{u}", tag=f"last{u}" if s == SLOT_TILES - 1 else f"pairs{s}_{u}", align_bytes=64) for s in range(SLOT_TILES) for u in range(2)}
 
-        def gated_expert(s):
+        sums = {}
+        halves = {}
+
+        def expert_passes(s, lo, hi):
             e, h = divmod(s, TILES_PER_EXPERT)
-            y = banks.tile([P, N], F32, name="y", tag=f"bank{h}")
+            if lo == 0:
+                sums[s] = banks.tile([P, N], F32, name="y", tag=f"bank{h}")
             order = list(range(PASSES))
             if s == SLOT_TILES - 1:
                 order = order[-1:] + order[:-1]
-            for a in order:
+            for a in order[lo:hi]:
                 nc.tensor.matmul_mx(
-                    out=y[:],
+                    out=sums[s][:],
                     lhsT=x_gathered[a][:, s * P : (s + 1) * P].bitcast(FP8X4),
                     lhsT_scale=(x_planes[:, a, :] if a < PASSES - 1 else x_last_plane[:])[:, s * P : (s + 1) * P],
                     rhs=w_pass[e][a].bitcast(FP4X4),
@@ -187,20 +191,22 @@ def tile_moe_nxt_lin_none_kernel(
                     start=(a == order[0]),
                     stop=(a == order[-1]),
                 )
-            y_by_u = y[:].rearrange("s (p u d) -> s u p d", u=2, d=2)
-            halves = []
+
+        def gate_tile(s):
+            y_by_u = sums[s][:].rearrange("s (p u d) -> s u p d", u=2, d=2)
             for u in range(2):
-                half = keep.tile([P, 2 * P], BF16, name=f"c_by_slot{s}_{u}", align_bytes=64)
-                rounded = half[:].rearrange("s (p d) -> s p d", d=2)
+                halves[s, u] = keep.tile([P, 2 * P], BF16, name=f"c_by_slot{s}_{u}", align_bytes=64)
+                rounded = halves[s, u][:].rearrange("s (p d) -> s p d", d=2)
                 if s == 1:
                     nc.vector.tensor_scalar(rounded, y_by_u[:, u], gate_col[:, s : s + 1], None, mybir.AluOpType.mult)
                 else:
                     nc.scalar.activation(rounded, y_by_u[:, u], COPY, scale=gate_col[:, s : s + 1])
-                halves.append(half)
-            for u in range(2):
-                pairs = turned.tile([P, P], F32, name="pairs", tag="pairs")
-                nc.tensor.transpose(pairs[:], halves[u][:].bitcast(F32), ident[:])
-                nc.scalar.copy(c_pairs[s, u][:], pairs[:])
+
+        def turn(s, u):
+            pairs = turned.tile([P, P], F32, name="pairs", tag="pairs")
+            nc.tensor.transpose(pairs[:], halves[s, u][:].bitcast(F32), ident[:])
+            nc.scalar.copy(c_pairs[s, u][:], pairs[:])
+            scatter(u, s, s + 1)
 
         def scatter(u, lo, hi):
             e, h = divmod(lo, TILES_PER_EXPERT)
@@ -222,10 +228,18 @@ def tile_moe_nxt_lin_none_kernel(
                 in_=wp_bf[:].rearrange("p f j -> p (f j)"),
             )
 
-        for s in range(SLOT_TILES):
-            gated_expert(s)
-            scatter(0, s, s + 1)
-            scatter(1, s, s + 1)
+        for s in range(SLOT_TILES - 1):
+            expert_passes(s, 0, PASSES)
+            gate_tile(s)
+            for u in range(2 if s < 2 else 0):
+                turn(s, u)
+        expert_passes(3, 0, PASSES - 1)
+        for u in range(2):
+            turn(2, u)
+        expert_passes(3, PASSES - 1, PASSES)
+        gate_tile(3)
+        for u in range(2):
+            turn(3, u)
         for f in range(FEATURE_TILES):
             quantise_wp(f, f + 1)
 

from contextlib import ExitStack

import concourse.mybir as mybir
from concourse.masks import make_identity

K, T, E, C, N, M = 2560, 640, 2, 256, 512, 384
FLOPS = 2 * K * N * E * C + 2 * N * M * T

F32 = mybir.dt.float32
BF16 = mybir.dt.bfloat16
I32 = mybir.dt.int32
U32 = mybir.dt.uint32
U16 = mybir.dt.uint16
U8 = mybir.dt.uint8
FP8X4 = mybir.dt.float8_e4m3fn_x4
FP4X4 = mybir.dt.float4_e2m1fn_x4
COPY = mybir.ActivationFunctionType.Copy

P = 128
PACK = 4
PASSES = K // (P * PACK)
TILES_PER_EXPERT = C // P
SLOT_TILES = E * TILES_PER_EXPERT
FEATURE_TILES = M // P
TOKEN_TILES = T // P
BANKS = 6
LIST_COLS = P // 16

X_FIRST = 2
W_FIRST = 3
W1_FIRST = 3
WARM = 2
STORE_GROUPS = (((0,), (1, 2)), ((0,), (1,), (2,)), ((0,), (1,), (2,)))
DOUBLED = ((0, 384), (384, 640))
XS_FIRST = P - 16 * PASSES
VCOPY = ((2, 0), (2, 2))
TOKEN_RUNS = ((0, 128), (128, 384), (384, 640))
QUADRANTS = (0, 2, 1, 3)
SCALE_PAD = 64


def tile_moe_nxt_lin_none_kernel(
    tc, x_words, x_scales, w_words, w_scales, wp, gate, offs, out
):
    nc = tc.nc
    with ExitStack() as ctx:
        keep = ctx.enter_context(tc.tile_pool(name="keep", bufs=1))
        banks = ctx.enter_context(tc.psum_pool(name="banks", bufs=1))
        turned = ctx.enter_context(tc.psum_pool(name="turned", bufs=4))

        def zero(planes, engine):
            engine.memset(planes.rearrange("p a n -> p (a n)").bitcast(I32), 0)

        def slot_offsets(lo, hi):
            return offsets[:, lo * LIST_COLS : hi * LIST_COLS]

        def load_weight_scales(e, queue):
            for r in range(4):
                queue.dma_start(
                    w_planes[e][r:P:32, :, :].bitcast(I32),
                    w_scales[e, :, r:16:4, :].rearrange("a q n -> q a n").bitcast(I32),
                )

        def move_token_scales():
            for q in QUADRANTS:
                first = XS_FIRST + 16 + 16 * q
                nc.sync.dma_start(
                    x_planes[32 * q : 32 * q + 4, :, :].bitcast(I32),
                    xs_gathered[first : first + 16, :].bitcast(I32),
                )

        def move_last_pass_scales():
            for r in range(4):
                nc.sync.dma_start(
                    x_last_plane[r:P:32, :].bitcast(I32),
                    xs_gathered[XS_FIRST + r : XS_FIRST + 16 : 4, :].bitcast(I32),
                )

        def load_weights(e, lo, hi):
            w_sb = keep.tile([P, hi - lo, 2 * N], U8, name=f"w_sb{e}_{lo}", align_bytes=64)
            nc.sync.dma_start(w_sb[:].bitcast(I32), w_words[e, lo:hi].rearrange("a p n -> p a n").bitcast(I32))
            w_pass[e].extend(w_sb[:, a, :] for a in range(hi - lo))

        w_planes = [keep.tile([P, PASSES, N], U8, name=f"w_planes{e}", align_bytes=64) for e in range(E)]
        x_planes = keep.tile([P, PASSES - 1, E * C], U8, name="x_planes", align_bytes=64)
        x_last_plane = keep.tile([P, E * C], U8, name="x_last_plane", align_bytes=64)
        w_pass = [[] for e in range(E)]
        windows = [keep.tile([P, T], F32, name=f"window{u}") for u in range(2)]
        gate_rows = keep.tile([P, P], F32, name="gate_rows")
        zero_col = keep.tile([P, 1], F32, name="zero_col")
        xs_window = keep.tile([P, T + SCALE_PAD], U8, name="xs_window")
        offsets = keep.tile([P, SLOT_TILES * LIST_COLS], U16, name="offsets")
        nc.sync.dma_start(
            xs_window[XS_FIRST + 16 :, :T].bitcast(I32),
            x_scales[: PASSES - 1].rearrange("a q t -> q a t").bitcast(I32),
        )
        nc.sync.dma_start(offsets[:], offs)
        nc.scalar.dma_start(xs_window[XS_FIRST : XS_FIRST + 16, :T].bitcast(I32), x_scales[PASSES - 1].bitcast(I32))
        zero(w_planes[0][:], nc.vector)
        nc.scalar.dma_start(gate_rows[P - SLOT_TILES :, :], gate[0].rearrange("(s p) -> s p", p=P))
        load_weight_scales(0, nc.scalar)
        nc.vector.memset(gate_rows[: P - SLOT_TILES, :], 0.0)
        nc.vector.memset(xs_window[:XS_FIRST, :T].bitcast(I32), 0)
        nc.vector.memset(xs_window[:, T:].bitcast(I32), 0)
        zero(x_planes[:], nc.vector)
        nc.vector.memset(x_last_plane[:].bitcast(I32), 0)
        nc.vector.memset(zero_col[:], 0.0)
        ident = keep.tile([P, P], F32, name="ident")
        make_identity(nc, ident[:])
        zero(w_planes[1][:], nc.vector)
        for window in windows:
            nc.scalar.copy(window[:], zero_col[:].to_broadcast([P, T]))

        x_pass = []

        def load_tokens(lo, hi):
            x_sb = keep.tile([P, (hi - lo) * T], U32, name=f"x_sb{lo}")
            nc.sync.dma_start(
                x_sb[:].bitcast(I32).rearrange("p (a t) -> p a t", t=T),
                x_words[lo:hi].rearrange("a p t r -> p a (t r)").bitcast(I32),
            )
            for a in range(lo, hi):
                over = SCALE_PAD if a == 0 else 0
                x_pass.append(x_sb[:, (a - lo) * T : (a - lo + 1) * T + over])

        load_tokens(0, X_FIRST)
        load_tokens(X_FIRST, W_FIRST)

        xs_gathered = keep.tile([P, E * C], U8, name="xs_gathered", align_bytes=64)
        nc.vector.tensor_copy(xs_gathered[:], xs_window[:].indirect(offsets[:]))
        gate_turned = banks.tile([P, P], F32, name="gate_turned", tag="bank3")
        nc.tensor.transpose(gate_turned[:], gate_rows[:], ident[:])
        gate_col = keep.tile([P, SLOT_TILES], F32, name="gate_col")
        nc.scalar.copy(gate_col[:], gate_turned[:, P - SLOT_TILES :])
        load_weights(0, 0, W_FIRST)
        move_token_scales()
        load_tokens(W_FIRST, PASSES)
        load_weights(0, W_FIRST, PASSES)
        move_last_pass_scales()
        load_weights(1, 0, W1_FIRST)
        load_weight_scales(1, nc.sync)
        load_weights(1, W1_FIRST, PASSES)
        wp_raw = keep.tile([P, PACK, M], F32, name="wp_raw")
        nc.sync.dma_start(wp_raw[:], wp.rearrange("(p j) f -> p j f", j=PACK))

        x_gathered = [keep.tile([P, E * C], U32, name=f"x_gathered{a}", align_bytes=64) for a in range(PASSES)]

        def gather_words(e, a):
            slots = slot_offsets(e * TILES_PER_EXPERT, (e + 1) * TILES_PER_EXPERT)
            nc.vector.tensor_copy(x_gathered[a][:, e * C : (e + 1) * C], x_pass[a].indirect(slots))

        nc.vector.tensor_copy(x_gathered[0][:], x_pass[0].indirect(offsets[:]))
        for e in range(E):
            gather_words(e, 1)
        for lo, hi in ((X_FIRST, W_FIRST), (W_FIRST, PASSES)):
            for e in range(E):
                for a in range(lo, hi):
                    gather_words(e, a)

        warm = banks.tile([P, N], F32, name="warm", tag="bank2")
        for i in range(WARM):
            nc.tensor.matmul_mx(
                out=warm[:],
                lhsT=x_gathered[X_FIRST - 1][:, :P].bitcast(FP8X4),
                lhsT_scale=xs_gathered[:, :P],
                rhs=x_gathered[0][:].bitcast(FP8X4),
                rhs_scale=xs_gathered[:],
                start=True,
                stop=True,
            )

        c_pairs = {(s, u): keep.tile([P, P], F32, name=f"c_pairs{s}_{u}", tag=f"last{u}" if s == SLOT_TILES - 1 else f"pairs{s}_{u}", align_bytes=64) for s in range(SLOT_TILES) for u in range(2)}

        sums = {}
        halves = {}

        def expert_passes(s, lo, hi):
            e, h = divmod(s, TILES_PER_EXPERT)
            if lo == 0:
                sums[s] = banks.tile([P, N], F32, name="y", tag=f"bank{h}")
            order = list(range(PASSES))
            if s == SLOT_TILES - 1:
                order = order[-1:] + order[:-1]
            for a in order[lo:hi]:
                nc.tensor.matmul_mx(
                    out=sums[s][:],
                    lhsT=x_gathered[a][:, s * P : (s + 1) * P].bitcast(FP8X4),
                    lhsT_scale=(x_planes[:, a, :] if a < PASSES - 1 else x_last_plane[:])[:, s * P : (s + 1) * P],
                    rhs=w_pass[e][a].bitcast(FP4X4),
                    rhs_scale=w_planes[e][:, a, :],
                    start=(a == order[0]),
                    stop=(a == order[-1]),
                )

        def gate_tile(s):
            y_by_u = sums[s][:].rearrange("s (p u d) -> s u p d", u=2, d=2)
            for u in range(2):
                halves[s, u] = keep.tile([P, 2 * P], BF16, name=f"c_by_slot{s}_{u}", align_bytes=64)
                rounded = halves[s, u][:].rearrange("s (p d) -> s p d", d=2)
                if s == 1:
                    nc.vector.tensor_scalar(rounded, y_by_u[:, u], gate_col[:, s : s + 1], None, mybir.AluOpType.mult)
                else:
                    nc.scalar.activation(rounded, y_by_u[:, u], COPY, scale=gate_col[:, s : s + 1])

        def turn(s, u):
            pairs = turned.tile([P, P], F32, name="pairs", tag="pairs")
            nc.tensor.transpose(pairs[:], halves[s, u][:].bitcast(F32), ident[:])
            nc.scalar.copy(c_pairs[s, u][:], pairs[:])
            scatter(u, s, s + 1)

        def scatter(u, lo, hi):
            e, h = divmod(lo, TILES_PER_EXPERT)
            nc.vector.tensor_copy(
                windows[u][:].indirect(slot_offsets(lo, hi)), c_pairs[lo, u][:]
            )

        wp_codes = {}
        wp_scales = keep.tile([P, M], U8, name="wp_scales", align_bytes=64)

        def quantise_wp(lo, hi):
            cols = slice(lo * P, hi * P)
            wp_bf = keep.tile([P, (hi - lo) * P, PACK], BF16, name=f"wp_bf{lo}", align_bytes=64)
            nc.scalar.copy(wp_bf[:], wp_raw[:, :, cols].rearrange("p j f -> p f j"))
            wp_codes[lo] = keep.tile([P, P], U32, name=f"wp_codes{lo}", tag=("wp0", "last1", "last0")[lo], align_bytes=64)
            nc.vector.quantize_mx(
                out=wp_codes[lo][:].bitcast(FP8X4),
                scales=wp_scales[:, cols],
                in_=wp_bf[:].rearrange("p f j -> p (f j)"),
            )

        for s in range(SLOT_TILES - 1):
            expert_passes(s, 0, PASSES)
            gate_tile(s)
            for u in range(2 if s < 2 else 0):
                turn(s, u)
        expert_passes(3, 0, PASSES - 1)
        for u in range(2):
            turn(2, u)
        expert_passes(3, PASSES - 1, PASSES)
        gate_tile(3)
        for u in range(2):
            turn(3, u)
        for f in range(FEATURE_TILES):
            quantise_wp(f, f + 1)

        c_all = keep.tile([P, T * PACK], BF16, name="c_all", align_bytes=64)
        c_by_token = [c_all[:, lo * PACK : hi * PACK] for lo, hi in TOKEN_RUNS]
        words = c_all[:].bitcast(F32).rearrange("p (t u) -> p t u", u=2)
        c_words = [words[:, lo:hi, :] for lo, hi in TOKEN_RUNS]
        for lo, hi in DOUBLED:
            nc.scalar.copy(words[:, lo:hi, :], windows[0][:, lo:hi].unsqueeze(2).to_broadcast([P, hi - lo, 2]))

        def weave(i):
            lo, hi = TOKEN_RUNS[i]
            nc.vector.tensor_copy(c_words[i][:, :, 1], windows[1][:, lo:hi])

        def project(i):
            lo, hi = TOKEN_RUNS[i]
            codes = keep.tile([P, hi - lo], U32, name=f"c_codes{i}", align_bytes=64)
            scales = keep.tile([P, hi - lo], U8, name=f"c_scales{i}", align_bytes=64)
            nc.vector.quantize_mx(out=codes[:].bitcast(FP8X4), scales=scales[:], in_=c_by_token[i])
            for group in STORE_GROUPS[i]:
                n = len(stored)
                stored.append(group)
                shape = [P, len(group), hi - lo]
                if n < 4:
                    o = banks.tile(shape, F32, name="o", tag=f"bank{(n + 2) % 4}")
                else:
                    o = turned.tile(shape, F32, name="o", tag="pairs")
                for j, f in enumerate(group):
                    cols = slice(f * P, (f + 1) * P)
                    nc.tensor.matmul_mx(
                        out=o[:, j, :],
                        lhsT=wp_codes[f][:].bitcast(FP8X4),
                        lhsT_scale=wp_scales[:, cols],
                        rhs=codes[:].bitcast(FP8X4),
                        rhs_scale=scales[:],
                        start=True,
                        stop=True,
                    )
                o_sb = keep.tile(shape, F32, name=f"o_sb{n}")
                (nc.vector.tensor_copy if (i, group[0]) in VCOPY else nc.scalar.copy)(o_sb[:], o[:])
                rows = out[group[0] * P : (group[-1] + 1) * P, lo:hi]
                nc.sync.dma_start(rows.rearrange("(f p) t -> p f t", p=P), o_sb[:])

        stored = []
        weave(0)
        for i in range(len(TOKEN_RUNS)):
            if i + 1 < len(TOKEN_RUNS):
                weave(i + 1)
            project(i)
